import numpy as np, ml_dtypes
CORES = [2,3,42,43,82,83,122,123]
N = 8
BF = ml_dtypes.bfloat16
def gentries(a):
    return np.ascontiguousarray(a.reshape(8, 16, -1).transpose(0, 2, 1)).reshape(8, -1)
def gtable(e):
    e = np.asarray(e); return np.ascontiguousarray(e.reshape(8, -1, 16).transpose(0, 2, 1)).reshape(128, -1).astype(np.int32)
K, C, NS, RO = 256, 2, 1024, 4
V, W = C * K, N * C * K
def parts(rng):
    lev = rng.integers(0, 160, (N, 8, 1, W)); b = lev + ((256 - lev) * rng.random((N, 8, 16, W))).astype(np.int64)
    L = rng.integers(0, W, (N, 8, 16, NS)); S = rng.integers(0, W, (N, 8, 16, V))
    P = np.argsort(rng.random((N, 8, C, NS)), axis=-1)[..., :K].reshape(N, 8, V); Q = rng.integers(0, NS, (N, 8, V))
    return np.minimum(b, 255), L, S, P, Q, rng.integers(400, 2000, (N, 8, 16, 1)), rng.integers(1600, 2900, (N, 8, 1))
def pack(b, L, S, P, Q, th, mg):
    return {"base": np.ascontiguousarray(b.reshape(N, 128, W)).astype(np.float32).astype(BF), "favor": np.ascontiguousarray(L.reshape(N, 128, NS)).astype(np.int32),
            "src": np.ascontiguousarray(S.reshape(N, 128, V)).astype(np.int32), "grant": np.stack([gtable(a) for a in P]), "part": np.stack([gtable(a) for a in Q]),
            "th": np.ascontiguousarray(th.reshape(N, 128, 1)).astype(np.int32), "mg": mg.astype(np.int32)}
def setup_inputs(rng):
    return pack(*parts(rng))
def setup_inputs_spread(rng):
    b, L, S, P, Q, th, mg = parts(rng)
    b = np.minimum((256 * rng.random((N, 8, 16, W)) * np.exp2(-rng.integers(0, 8, (N, 8, 1, W)).astype(np.float64))).astype(np.int64), 255)
    L = np.minimum((W * rng.random(L.shape) ** 3).astype(np.int64), W - 1); S = np.minimum((W * rng.random(S.shape) ** 2).astype(np.int64), W - 1)
    Q = np.minimum((NS * rng.random(Q.shape) ** 3).astype(np.int64), NS - 1)
    th = np.minimum(np.exp2(12 * rng.random(th.shape)).astype(np.int64) - 1, 4079); mg = np.minimum(np.exp2(12 * rng.random(mg.shape)).astype(np.int64) - 1, 4079)
    return pack(b, L, S, P, Q, th, mg)
def setup_inputs_ends(rng):
    b, L, S, P, Q, th, mg = parts(rng)
    def tip(x, lo, hi, share):
        m = rng.random(x.shape); return np.where(m < 0.5 * share, lo, np.where(m < share, hi, x))
    sort_ = rng.integers(0, 5, (N, 8, 1, W)); el = 255 * rng.integers(0, 2, b.shape)
    b = np.where(sort_ == 0, 0, np.where(sort_ == 1, 255, np.where(sort_ < 4, el, tip(b, 0, 255, 0.5))))
    L = tip(L, 0, W - 1, 0.7); S = tip(S, 0, W - 1, 0.7); Q = tip(Q, 0, NS - 1, 0.8)
    ix = np.concatenate([np.arange(K // 2), np.arange(NS - K // 2, NS)]); P = rng.permuted(np.tile(ix, (N, 8, C, 1)), axis=-1).reshape(N, 8, V)
    th = tip(th, 0, 4079, 1.0); th[:, :, 15] = 4079; th[:, :, 0] = 0
    for r in range(N):
        last = 4079 if (N - 1 - r) % 2 == 0 else 0
        mg[r, :7, 0] = rng.permutation(np.array([0, 0, 0, 4079, 4079, 4079, 4079 - last])); mg[r, 7, 0] = last
    zero = rng.random((N, 8)) < 0.7; zero[:, 7] = True
    b[..., W - 1] = np.where(zero[:, :, None], 0, b[..., W - 1])
    hi = np.array([0, K + 1, K - 2, 2 * K - 1, V - 1, V - 2 - K]); lo = np.array([K, 1, 2 * K - 2, K - 1, V - 2, V - 1 - K])
    b[:, :, :, hi] = 255; b[:, :, :, lo] = 0; S[:, :, 15, hi] = W - 1; S[:, :, 15, lo] = 0
    np.put_along_axis(L[:, :, 15], P[:, :, hi], W - 1, 2)
    return pack(b, L, S, P, Q, th, mg)
def setup_inputs_corners(rng):
    b, L, S, P, Q, th, mg = parts(rng); e = np.arange(V); rev = (e // K ^ 1) * K + e % K
    for r in range(N):
        for g, k in enumerate(rng.permutation(8)):
            if k == 0: S[r, g] = e
            if k == 1:
                L[r, g] = rng.integers(0, W, (1, NS)); S[r, g] = rng.choice(np.array([0, V - 1, V, W - 1]), (16, V)); Q[r, g] = rng.choice(np.array([0, NS - 1]), V)
            if k == 2:
                b[r, g] = rng.integers(0, 4, (16, W)); th[r, g, :, 0] = rng.integers(0, 41, 16); mg[r, g, 0] = rng.integers(0, 21)
            if k == 3:
                Q[r, g] = P[r, g]; S[r, g] = rev; mg[r, g, 0] = rng.integers(0, 600)
                for c in range(C):
                    a = e[c * K:(c + 1) * K]; L[r, g][:, P[r, g, a]] = np.where(rng.random((16, K)) < 0.5, a, rev[a])
            if k == 4:
                L[r, g] = rng.integers(V, W, (16, NS)); S[r, g] = rng.integers(V, W, (16, V)); th[r, g] = 4079; mg[r, g] = 4079
            if k == 5: th[r, g] = 0; mg[r, g] = 0
            if k == 6:
                b[r, g] = 255 * rng.integers(0, 2, (16, W)); L[r, g, 8:] = L[r, g, :8]; th[r, g, :, 0] = 255 * rng.integers(0, 16, 16); mg[r, g, 0] = 255 * rng.integers(0, 9)
            if k == 7:
                b[r, g] = 8 * rng.integers(0, 32, (1, W)); th[r, g, :, 0] = 128 * rng.integers(1, 20, 16); mg[r, g, 0] = 128 * rng.integers(4, 14)
    return pack(b, L, S, P, Q, th, mg)
def setup_inputs_crowd(rng):
    b, L, S, P, Q, th, mg = parts(rng); z = (1 + (RO - 1) % (N - 1)) * V + ((RO - 1) % C) * K
    s = 490 + np.arange(64); low = (s // 16)[None, :] + (np.arange(16)[:, None] < (s % 16)[None, :]).astype(np.int64)
    for r in range(N):
        for g, k in enumerate(rng.permutation(8) % 4):
            if k == 3: continue
            b[r, g, :, :V] = rng.integers(200, 256, (16, V)); b[r, g, :, z:z + 64] = low; b[r, g, :, z + 64:z + K] = 0
            L[r, g] = z + K - 1 if k == 2 else rng.integers(z + 64, z + K, (16, NS))
            if k == 2: Q[r, g] = rng.integers(0, NS)
            c0 = (1, 0, C - 1)[k]; a = int(rng.integers(0, K)) + K * np.arange(c0, C)
            b[r, g][:, a] = 0; S[r, g][:, a] = z + rng.integers(0, 64, (16, C - c0))
            th[r, g, :, 0] = rng.integers(480, 521, 16); mg[r, g, 0] = rng.choice(np.array([0, 1, 3199]))
    return pack(b, L, S, P, Q, th, mg)
def check_inputs(d):
    bad = []; x = np.asarray(d["base"]).astype(np.float32)
    if not np.all((x >= 0) & (x <= 255) & (x == np.floor(x))): bad.append("range of base")
    for k, lo, hi in (("favor", 0, W - 1), ("src", 0, W - 1), ("grant", 0, NS - 1), ("part", 0, NS - 1), ("th", 0, 4079), ("mg", 0, 4079)):
        if np.min(d[k]) < lo or np.max(d[k]) > hi: bad.append("range of " + k)
    p = np.sort(np.stack([gentries(a) for a in d["grant"]]).astype(np.int64).reshape(N, 8, C, K), axis=-1)
    if np.any(p[..., 1:] == p[..., :-1]): bad.append("grantors of a class differ")
    return bad
def reference(base, favor, src, grant, part, th, mg):
    b = base.astype(np.float32).astype(np.int64).reshape(N, 8, 16, W); X = b + 0
    L = favor.astype(np.int64).reshape(N, 8, 16, NS); S = src.astype(np.int64).reshape(N, 8, 16, V)
    P = np.stack([gentries(a) for a in grant]).astype(np.int64); Q = np.stack([gentries(a) for a in part]).astype(np.int64)
    lim = th.astype(np.int64).reshape(N, 8, 16, 1); gap = mg.astype(np.int64).reshape(N, 8, 1); A = np.zeros((N, 8), np.int64); lane = np.arange(K)
    for t in range(RO):
        c = t % C; o = c * K; v = (c ^ 1) * K; e = o + lane; be = b[..., o:o + K]; old = X[..., o:o + K] + 0; s = S[..., o:o + K] + 0
        far = np.take_along_axis(X, s.reshape(N, 8, 1, 16 * K), 3).reshape(N, 8, 16, 16, K)
        dist = np.sum(np.abs(far - old[:, :, :, None, :]), axis=2)
        lapse = dist > lim + (A & 31)[:, :, None, None]
        x = np.where(lapse, be, old); s = np.where(lapse, e, s)
        pe = P[:, :, None, o:o + K]; T = np.take_along_axis(L, pe, 3)
        y = np.take_along_axis(X, T.reshape(N, 8, 1, 16 * K), 3).reshape(N, 8, 16, 16, K)
        k1 = np.argmin(y, axis=3); least = np.min(y, axis=3); less = least < x
        x = np.where(less, least, x); s = np.where(less, np.take_along_axis(T, k1, 2), s)
        den = np.sum(be - x, axis=2) - np.sum(b[..., v:v + K] - X[..., v:v + K], axis=2) > gap
        k2 = np.sum(y[:, :, :, 0, :], axis=2) & 15
        new = np.take_along_axis(np.take_along_axis(L, Q[:, :, None, o:o + K], 3), k2[:, :, None, :], 2)
        put = den[:, :, None, :] & (np.arange(16)[:, None] == ((lane + t) & 15)[None, :])
        np.put_along_axis(L, np.broadcast_to(pe, T.shape), np.where(put, new, T), 3)
        x = np.where(den[:, :, None, :], be, x); s = np.where(den[:, :, None, :], e, s); A = A + np.sum(den, axis=2)
        d = 1 + t % (N - 1)
        X[..., o:o + K] = x; S[..., o:o + K] = s; X[..., d * V + o:d * V + o + K] = np.roll(x, d, axis=0)
    return {"yx": X.reshape(N, 128, W).astype(np.float32).astype(BF), "ys": S.reshape(N, 128, V).astype(np.float32), "yl": L.reshape(N, 128, NS).astype(np.float32)}

@@ -1,0 +1,602 @@
+from concourse.bass import DstId, RemoteDMATransfer
+from concourse.mybir import dt, AluOpType, AxisListType, ActivationFunctionType
+
+K, V, WN, NS, RO = 256, 512, 4096, 1024, 4
+CH = [(0, 192), (192, 64)]
+G1 = [(0, 32, "a"), (32, 64, "a"), (64, 96, "a"), (96, 128, "a"), (128, 144, "a"), (144, 192, "v"), (192, 224, "a"), (224, 256, "a")]
+BASE_CH = [(0, 1024), (1024, 1024), (2048, 1024), (3072, 512), (3584, 512)]
+GA = [(0, 256)]
+MAGIC_S, FASTX, FASTP, KOACT, VUPD, LOOK = True, True, True, True, True, 0.5
+E17 = 2.0 ** -17
+D0W = 1536
+
+SCRATCH = {
+    "XB": ("sbuf", [128, WN], "bfloat16"), "XS": ("sbuf", [128, RO * K], "bfloat16"), "LAND": ("sbuf", [128, RO * K], "bfloat16"),
+    "WW": ("sbuf", [128, WN], "float32"), "LI": ("sbuf", [128, NS], "int32"), "LF": ("sbuf", [128, NS], "float32"),
+    "SI": ("sbuf", [128, V], "int32"), "SU": ("sbuf", [128, RO * K], "uint16"), "SF": ("sbuf", [128, V], "float32"),
+    "PI": ("sbuf", [128, 32], "int32"), "QI": ("sbuf", [128, 32], "int32"), "PU": ("sbuf", [128, 32], "uint16"), "QU": ("sbuf", [128, 32], "uint16"),
+    "AA": ("sbuf", [128, WN], "bfloat16"), "AB": ("sbuf", [128, WN], "bfloat16"),
+    "YA": ("sbuf", [128, 2048], "float32"), "YB": ("sbuf", [128, 2048], "float32"), "SC": ("sbuf", [128, 2048], "float32"),
+    "D0": ("sbuf", [128, D0W], "bfloat16"), "TF": ("sbuf", [128, K], "float32"),
+    "TU": ("sbuf", [128, K], "uint16"), "KO": ("sbuf", [128, RO * K], "float32"), "MM": ("sbuf", [128, K], "float32"),
+    "K3": ("sbuf", [128, K], "float32"), "K4": ("sbuf", [128, K], "float32"), "KT": ("sbuf", [128, K], "float32"), "X2": ("sbuf", [128, K], "bfloat16"),
+    "Y0": ("sbuf", [128, K], "bfloat16"), "HM": ("sbuf", [128, K], "float32"), "GG": ("sbuf", [128, K], "float32"),
+    "SG": ("sbuf", [128, K], "float32"), "PT": ("sbuf", [128, K], "float32"), "DM": ("sbuf", [128, K], "float32"),
+    "I1": ("sbuf", [128, K], "int32"), "I2": ("sbuf", [128, K], "int32"),
+    "BT": ("sbuf", [128, RO * K], "bfloat16"), "CNT": ("sbuf", [128, 16], "float32"),
+    "KJ": ("sbuf", [128, 260], "int32"), "KA": ("sbuf", [128, 260], "int32"), "ND": ("sbuf", [128, 260], "bfloat16"),
+    "BK": ("sbuf", [128, 128], "int32"), "MR": ("sbuf", [128, 128], "float32"), "SB": ("sbuf", [128, 128], "float32"), "SB2": ("sbuf", [128, 128], "float32"),
+    "SLI": ("sbuf", [128, 512], "int32"), "SEL": ("sbuf", [128, 512], "bfloat16"), "B8": ("sbuf", [128, 128], "int32"),
+    "IB": ("sbuf", [128, 128], "bfloat16"), "IBN": ("sbuf", [128, 128], "bfloat16"), "IF": ("sbuf", [128, 128], "float32"), "IFN": ("sbuf", [128, 128], "float32"),
+    "BP": ("sbuf", [128, 128], "bfloat16"), "BN": ("sbuf", [128, 128], "bfloat16"), "BF": ("sbuf", [128, 128], "float32"),
+    "CC": ("sbuf", [128, 288], "bfloat16"), "PM": ("sbuf", [128, 512], "float32"), "FF": ("sbuf", [128, 512], "bfloat16"), "FL": ("sbuf", [128, 128], "bfloat16"),
+    "ONE": ("sbuf", [128, K], "bfloat16"), "RW": ("sbuf", [128, 11 * 128], "bfloat16"),
+    "THI": ("sbuf", [128, 4], "int32"), "MGI": ("sbuf", [128, 4], "int32"), "CI": ("sbuf", [128, 16], "int32"), "CF": ("sbuf", [128, 16], "float32"),
+    "DH": ("sbuf", [128, 128], "bfloat16"), "DL": ("sbuf", [128, RO * 128], "bfloat16"), "MH": ("sbuf", [128, 128], "bfloat16"), "DB": ("sbuf", [128, K], "bfloat16"),
+    "FI": ("sbuf", [128, 128], "float32"), "FR": ("sbuf", [128, 384], "float32"), "BFN": ("sbuf", [128, 128], "float32"), "XT": ("sbuf", [128, K], "bfloat16"), "CJ": ("sbuf", [128, 16], "float32"),
+}
+for _b in ("PD0", "PD1", "PZ0", "PZ1", "PKB", "PM1", "PM2", "PM3"):
+    SCRATCH[_b] = ("psum", [128, 512], "float32")
+NDMA = 40
+SEMAPHORES = ["sv", "sa", "sp", "sg", "sent"] + ["dm%d" % i for i in range(NDMA)] + ["ar%d" % i for i in range(RO * len(CH))]
+ESZ = {"bfloat16": 2, "float16": 2, "uint16": 2, "float32": 4, "int32": 4}
+A = AluOpType
+FN = ActivationFunctionType
+COST = (1.0, 0.5, 1.56, 3.8, 90.0, 2600.0, 200.0)
+PERIOD = 1700
+SLOT = {k: int(x) for k, x in (y.split("=") for y in """
+PI:ia=-3000 LI:ia=-2999 SI:ia=-2998 XB:ia=-2997 XB:ib=-2996 XB:ic=-2995 XB:id=-2994 XB:ie=-2993 THI:ia=-2992 MGI:ia=-2991 THI:ib=-2990 QI:ia=-2989 SI:ib=-2988 ONE:ia=-2227 FL:ia=-2105 CC:ia=-2105 FF:ia=-2095 FL:ib=-2094 D0:ia=-2007 KA:ia=-1991 CI:ia=-1987 CF:ia=-1908 ND:ia=-1907 FF:ic=-1886 BF:ia=-1845 FL:ic=-1826 CF:ib=-1690 CF:id=-1626 RW:ic=-1467 MH:ia=-1448 PU:ia=-1392 FL:id=-1391 CF:ic=-1391 D0:ib=-1390 IB:ia=-1378 RW:ib=-1308 SB2:ia=-1270 FF:id=-1119 SB:ia=-1108 CF:ie=-999 PM:id=-971 PM:ic=-932 RW:ie=-929 RW:ij=-918 PM:ib=-914 PM:ia=-913 SU:ia=-913 PM3:ia=-912 LF:ia=-911 KO:ia=-911 PD:ia=-910 DB:ia=-910 WW:ib=-909 PKB:ia=-909 WW:id=-908 WW:if=-907 CI:ib=-906 CI:id=-897 CF:if=-875 CI:ie=-875 CI:ic=-874 CF:ih=-874 CF:ii=-874 MH:ib=-873 WW:ih=-872 QU:ia=-861 RW:ik=-840 FR:ia=-839 RW:id=-838 FR:ic=-838 FR:ib=-837 CC:ic=-817 MH:ic=-800 PD:ib=-769 PD:ic=-768 CF:ig=-742 PD:id=-717 CC:ib=-622 RW:ii=-610 FI:ia=-607 KJ:ia=-606 FF:ib=-594 BP:ia=-569 BN:ia=-569 RW:ia=-569 BFN:ia=-569 IBN:ia=-558 IF:ia=-548 WW:ia=-537 PD:ie=-520 TF:ra=-516 RW:ig=-207 WW:ic=-206 BK:ia=-172 B8:ia=-161 MR:ia=-140 B8:ib=-139 SLI:ia=-88 AA:g5a=-35 RW:ih=35 IFN:ia=36 WW:ie=36 PD:if=81 PD:ig=81 PD:ih=91 PM1:r0a=92 DH:ia=213 AA:g0a=224 WW:ig=224 DL:ia=236 BT:ib=236 BT:ia=237 AA:g1a=238 AA:g2a=238 AB:b0a=238 AB:b0b=239 AA:g3a=240 PD:ii=312 PD:ij=313 PD:ik=331 PD:il=332 PM3:c0a=333 PM2:ha=334 PD:b0a=334 PM1:r1a=335 PD:b0b=336 PD:b1a=367 AA:g4a=519 Y0:ha=528 AB:b1a=528 out:c0a=531 AB:b1b=548 PZ:b0a=628 AA:g6a=629 AB:b2a=630 PD:b1b=695 AB:b2b=750 AA:g7a=801 PM1:ha=816 out:c1a=862 TU:r0a=1031 PD:b2a=1086 PD:b2b=1090 PZ:b1a=1111 PD:b3a=1112 AB:b3a=1138 AB:b3b=1138 RW:if=1138 HM:ha=1139 SG:c0a=1139 PT:c0a=1139 SG:c1a=1139 CJ:ea=1141 SF:s0a=1142 out:s0a=1142 KO:s0a=1142 WW:u0b=1143 CF:ea=1143 DL:ea=1143 KO:s1a=1144 SF:s1a=1145 out:s1a=1156 out:s1c=1157 SEL:ia=1162 YA:r1a=1163 PZ:b2a=1163 PD:b3b=1163 PZ:c0b=1164 PZ:b3a=1165 PZ:c0c=1166 PM3:c0b=1166 PM2:hb=1167 PZ:c1b=1168 PZ:c1c=1168 PM3:c1a=1168 PM3:c1b=1179 PZ:s0a=1180 TU:r1a=1184 YB:c0a=1184 YB:c1a=1184 SC:c0a=1185 PZ:c0a=1185 MM:c0a=1186 K3:c0a=1186 SC:c1a=1186 X2:c0a=1187 MM:c1a=1188 GG:ha=1189 PZ:c1a=1189 KT:c0a=1190 K3:c1a=1190 K4:c0a=1191 out:ia=1193 PD:u0b=1197 X2:c1a=1202 out:ib=1202 PM3:ea=1218 PZ:s1a=1239 PZ:s0b=1240 PZ:s1b=1251 PD:u0a=1252 PD:u0c=1253 out:eb=1261 XS:c0a=1262 XT:c1a=1262 KT:c1a=1263 XS:c1a=1273 PT:c1a=1273 K4:c1a=1274 PM3:ka=1274 DM:c0a=1280 DM:c1a=1280 KO:ka=1281 SU:ka=1282 LF:c0a=1283 LF:c1a=1286 SU:s0a=1287 SU:s1a=1298 WW:u1a=1299 out:c0c=1342 out:ic=1343 out:c1c=1363 out:s1b=1363 out:ec=1364 out:ea=1384 PD:u0d=1543 out:c1b=1564 out:c0b=1565 WW:u0a=1566 BT:u0a=1931
+ONE:ia=-1841 FL:ia=-1840 MH:ia=-1679 FL:ib=-1549 D0:ia=-1458 KA:ia=-1426 CI:ia=-1406 CF:ia=-1405 FL:ic=-1404 CF:ic=-1403 CF:id=-1350 IB:ia=-1349 PU:ia=-1348 FF:ia=-1336 BF:ia=-1336 CC:ia=-1335 CF:ib=-1324 CF:ie=-1315 SB2:ia=-1314 FL:id=-1312 SB:ia=-1311 D0:ib=-1310 PM:ib=-1309 PM:ia=-1281 PM:id=-1210 FF:ic=-1209 PM:ic=-1208 FF:id=-1133 ND:ia=-932 PM3:ia=-932 LF:ia=-932 SU:ia=-931 KO:ia=-931 DB:ia=-930 SEL:ia=-929 PKB:ia=-928 TU:q0a=-928 WW:wb=-927 WW:wd=-926 CI:ib=-925 CI:id=-905 CI:ie=-905 CF:if=-904 CF:ih=-904 WW:wf=-904 WW:wh=-904 CI:ic=-903 CF:ii=-902 RW:ij=-888 QU:ia=-872 MH:ib=-721 RW:ih=-668 RW:ie=-667 RW:ig=-653 RW:ic=-652 FR:ia=-624 RW:ii=-623 FR:ib=-594 FR:ic=-589 RW:ik=-588 RW:ib=-587 RW:id=-586 IFN:ia=-583 IBN:ia=-582 TF:ra=-539 CC:ic=-501 CC:ib=-480 IF:ia=-441 BP:ia=-440 FI:ia=-213 KJ:ia=17 BK:ia=18 B8:ia=47 BFN:ia=119 BN:ia=128 RW:ia=128 TF:qa=129 WW:wa=130 WW:wc=130 WW:we=131 WW:wg=131 DH:ia=132 BT:ib=132 WW:wi=132 AA:g0a=162 BT:ia=163 DL:ia=202 AA:g1a=203 PZ:wa=237 PM1:r0a=238 AB:b0a=243 MR:ia=257 PM1:q0a=267 PZ:wb=268 PD:wa=268 B8:ib=279 PD:wb=310 PZ:wc=310 PD:wc=310 FF:ib=311 PZ:wd=311 PZ:we=311 PD:ic=312 PD:id=312 PM2:ha=312 PD:wd=312 PD:ia=313 PD:ib=313 PM3:c0a=314 PD:b0a=314 PM1:r1a=314 SLI:ia=322 out:c0a=322 out:c1a=323 PD:b0b=325 AA:g2a=359 AB:b0b=359 Y0:ha=360 PD:b1a=366 PZ:b0a=394 AA:g3a=401 AA:g4a=409 AB:b1a=410 AB:b1b=471 PM1:ha=495 AA:g6a=620 AB:b2a=720 PD:b1b=728 AB:b2b=741 AA:g7a=810 TU:r0a=812 AB:b3a=831 PD:b2a=908 PD:b2b=909 PZ:b1a=911 PD:b3a=911 PZ:b2a=952 CF:ig=1041 MH:ic=1042 out:c0c=1048 out:c1c=1049 AB:b3b=1077 YA:r1a=1122 HM:ha=1138 RW:if=1139 SG:c0a=1139 PT:c0a=1139 SG:c1a=1139 CJ:ea=1139 SF:s0a=1140 KO:s0a=1141 WW:u0b=1141 CF:ea=1141 DL:ea=1141 out:s0a=1142 KO:s1a=1142 PD:b3b=1154 out:eb=1156 PZ:c0b=1165 PZ:b3a=1165 out:ib=1165 PZ:c0c=1166 PM3:c0b=1166 out:ia=1166 PM2:hb=1167 PZ:c1b=1168 PZ:c1c=1168 PM3:c1a=1168 PM3:c1b=1168 PZ:s0a=1169 PD:u0b=1169 PM3:ea=1169 PZ:s1a=1170 SF:s1a=1175 PZ:s0b=1181 TU:r1a=1183 AA:g5a=1184 YB:c0a=1184 YB:c1a=1184 SC:c0a=1185 PZ:c0a=1185 MM:c0a=1186 K3:c0a=1186 SC:c1a=1186 X2:c0a=1187 MM:c1a=1187 out:s1b=1196 GG:ha=1198 out:ic=1209 out:ea=1210 out:ec=1211 out:s1a=1215 out:s1c=1216 PZ:c1a=1249 WW:u0a=1256 PZ:s1b=1261 KT:c0a=1274 K3:c1a=1274 K4:c0a=1275 X2:c1a=1275 XS:c0a=1276 XT:c1a=1276 KT:c1a=1276 XS:c1a=1277 PT:c1a=1277 out:c1b=1277 K4:c1a=1278 PM3:ka=1280 DM:c0a=1280 DM:c1a=1281 KO:ka=1281 SU:ka=1282 LF:c0a=1282 LF:c1a=1282 SU:s0a=1283 SU:s1a=1284 WW:u1a=1284 PD:u0a=1322 out:c0b=1329 BT:u0a=1881 PD:u0c=1968 PD:u0d=1969
+""".split())}
+URGENT = {}
+
+
+def plan(g, core, T, topo, cost=COST):
+    rank, n = T.rank_of(core), len(T.cores)
+    CYC, PEC, GAT, SCA, _, REM, _ = cost
+    ops, tag, seen = [], ["i", 0], {}
+
+    def v(name, lo=None, hi=None, step=1, p=(0, 128)):
+        if lo is None:
+            lo, hi = 0, SCRATCH[name][1][1]
+        ap = T[name][p[0]:p[1], lo:hi:step] if step != 1 else T[name][p[0]:p[1], lo:hi]
+        return {"ap": ap, "reg": [(name, lo, hi)], "n": len(range(lo, hi, step)), "sz": ESZ[SCRATCH[name][2]], "ps": SCRATCH[name][0] == "psum"}
+
+    def ind(win, off):
+        return {"ap": win["ap"].indirect(off["ap"]), "reg": win["reg"], "off": off["reg"], "n": 16 * off["n"], "sz": 4, "ps": False, "ind": True}
+
+    def add(eng, fn, outs, ins, dur, lat=0.0, kind="c", extra=None):
+        rd, wr = [], []
+        for x in ins:
+            if isinstance(x, dict):
+                rd += x["reg"] + x.get("off", [])
+        for x in outs:
+            wr += x["reg"]
+            rd += x.get("off", [])
+        ops.append({"eng": eng, "fn": fn, "rd": rd, "wr": wr, "dur": dur, "lat": lat, "kind": kind, "x": extra,
+                    "t": tag[1]})
+        key = "%s:%s" % (wr[0][0].rstrip("01") if wr and wr[0][0][:2] in ("PD", "PZ") else wr[0][0] if wr else "out", tag[0])
+        seen[key, tag[1]] = seen.get((key, tag[1]), -1) + 1
+        ops[-1]["tag"] = "%s%s" % (key, "abcdefghijklmnopqrstuvwxyz"[seen[key, tag[1]]])
+
+    def a_(x):
+        return x["ap"] if isinstance(x, dict) else x
+
+    def vcost(out, x, two=1.0):
+        if out.get("ind"):
+            return 50 + SCA * CYC * out["n"]
+        if x.get("ind"):
+            return 50 + GAT * CYC * x["n"]
+        return 30 + CYC * max(64, x["n"] * two * (0.5 if out["sz"] == 2 and x["sz"] == 2 and two == 1.0 else 1))
+
+    def ts(out, x, s1, op0, s2=None, op1=None):
+        if op1 is None:
+            fn = lambda: g.vector.tensor_scalar(out["ap"], x["ap"], a_(s1), None, op0)
+        else:
+            fn = lambda: g.vector.tensor_scalar(out["ap"], x["ap"], a_(s1), a_(s2), op0, op1)
+        add("v", fn, [out], [x, s1, s2], vcost(out, x))
+
+    def tt(out, x, y, op):
+        add("v", lambda: g.vector.tensor_tensor(out["ap"], x["ap"], y["ap"], op), [out], [x, y], vcost(out, x, 1.0001 if x["ps"] or y["ps"] else 2.0))
+
+    def cp(out, x):
+        add("v", lambda: g.vector.tensor_copy(out["ap"], x["ap"]), [out], [x], vcost(out, x))
+
+    def ms(out, c):
+        add("v", lambda: g.vector.memset(out["ap"], c), [out], [], vcost(out, out))
+
+    def act(out, x, func=FN.Identity, bias=0.0, scale=1.0, acc=None):
+        if acc is None:
+            fn = lambda: g.scalar.activation(out["ap"], x["ap"], func, bias=a_(bias), scale=a_(scale))
+        else:
+            fn = lambda: g.scalar.activation(out["ap"], x["ap"], func, bias=a_(bias), scale=a_(scale), accum_out=acc["ap"])
+        add("a", fn, [out] + ([acc] if acc else []), [x, bias, scale], 65 + CYC * max(64, x["n"] * (GAT if x.get("ind") else 1)))
+
+    def mm(out, terms, first=True, last=True):
+        def fn():
+            r = None
+            for i, (l, x) in enumerate(terms):
+                r = g.tensor.matmul(out["ap"], l["ap"], x["ap"], first and i == 0, last and i == len(terms) - 1)
+            return r
+        o = out if first and last else {"reg": [(out["reg"][0][0], 0, 512)]}
+        add("p", fn, [o], [y for t_ in terms for y in t_], sum(PEC * max(64, x["n"]) * (4 if x["sz"] == 4 else 1) for _, x in terms), lat=60.0,
+            kind="c" if first else "acc")
+
+    def iota(out, pat, base, cm):
+        if SCRATCH[out["reg"][0][0]][2] == "int32":
+            fn = lambda: g.iota(out["ap"], pat, base, cm)
+        else:
+            fn = lambda: g.iota(out["ap"], pat, base, cm, allow_small_or_imprecise_dtypes=True)
+        add("g", fn, [out], [], 130 + 2 * CYC * out["n"])
+
+    def dma(q, out, x, nbytes, after=None):
+        e = g.sync if q == "s" else g.scalar
+        add(q, lambda: e.dma_start(a_(out), a_(x)), [out] if isinstance(out, dict) else [], [x, after], 60.0, lat=1800.0, kind="d", extra=nbytes)
+
+    row = lambda i: v("RW", 128 * i, 128 * i + 128, p=(0, 1))
+    one1 = lambda w: v("ONE", 0, w, p=(0, 1))
+    cf = lambda i, p=(0, 128): v("CF", i, i + 1, p=p)
+    ci = lambda i, p=(0, 128): v("CI", i, i + 1, p=p)
+    IB, IBN, IF, IFN, BP, BN, BF = (v(x) for x in ("IB", "IBN", "IF", "IFN", "BP", "BN", "BF"))
+    WW, LF = v("WW"), v("LF")
+
+    dma("s", v("PI"), T.grant[:], 16384)
+    dma("s", v("LI"), T.favor[:], 524288)
+    dma("s", v("SI", 0, K), T.src[:, 0:K], 131072)
+    for j, (lo, w) in enumerate(BASE_CH):
+        dma("s", v("XB", lo, lo + w), T.base[:, lo:lo + w], 256 * w)
+    dma("s", v("THI", 0, 1), T.th[:], 8192)
+    dma("s", v("MGI", 0, 1, p=(0, 8)), T.mg[:], 512)
+    dma("s", v("THI", 2, 3, p=(32, 40)), T.mg[:], 512)
+    dma("s", v("QI"), T.part[:], 16384)
+    dma("s", v("SI", K, V), T.src[:, K:V], 131072)
+
+    iota(v("KJ"), [[-1, 260]], 1024, 1)
+    iota(v("BK"), [[-16, 8], [0, 16]], 0, 1)
+    iota(v("MR"), [[0, 8], [1, 16]], 0, 0)
+    ms(v("FF"), 0.0)
+    iota(v("FF", 0, 512, p=(0, 1)), [[0, 2], [1, 256]], 0, 0)
+    iota(v("SLI"), [[-1, 32], [0, 16]], 0, 1)
+    iota(v("B8", 0, 128, p=(0, 8)), [[-1, 8], [0, 16]], 0, 1)
+    iota(v("B8", 0, 128, p=(32, 40)), [[-1, 8], [0, 16]], 0, 1)
+    ms(v("FF", 0, 512, p=(32, 33)), 1.0)
+    ms(v("FF", 256, 512, p=(64, 65)), 1.0)
+    ms(v("FL"), 0.0)
+    for pp, c_ in ((0, E17), (32, -128.0), (64, 2.0 ** -9)):
+        ms(v("FL", 0, 128, p=(pp, pp + 1)), c_)
+    ms(v("ONE"), 1.0)
+    ts(IB, v("KJ", 0, 128), 1024.0, A.is_equal)
+    act(IBN, IB, scale=-1.0)
+    act(IF, IB)
+    act(IFN, IB, scale=-1.0)
+    ts(v("KA"), v("KJ"), 15, A.bitwise_and)
+    cp(cf(0), v("KA", 0, 1))
+    ts(v("ND"), v("KA"), 0.0, A.not_equal, -(2.0 ** 23), A.mult)
+    ts(BF, v("BK"), cf(0), A.is_equal)
+    act(BP, BF, scale=512.0)
+    act(BN, BF, scale=-512.0)
+    ms(v("CC"), 0.0)
+    act(v("CC", 15, 143, 16), v("BF", 0, 128, 16), scale=2048.0)
+    act(v("CC", 160, 288, 16), v("BF", 0, 128, 16), scale=2048.0)
+    ts(v("SB2"), v("MR"), cf(0), A.add, 1.0, A.add)
+    tt(v("SB"), v("SB2"), BF, A.mult)
+    ts(cf(1), cf(0), 8.0, A.is_lt)
+    ts(cf(2), cf(0), 8.0, A.is_ge)
+    ts(v("PM", 0, 128), v("SB"), 8.0, A.is_equal)
+    ts(v("PM", 128, 256), v("SB"), 16.0, A.is_equal, cf(1), A.mult)
+    ts(v("PM", 256, 384), v("SB"), 16.0, A.is_equal, cf(2), A.mult)
+    ts(v("PM", 384, 512), v("SB"), 24.0, A.is_equal)
+    ts(ci(0), v("KJ", 0, 1), 96, A.bitwise_and)
+    cp(cf(3), ci(0))
+    ts(v("SEL"), v("SLI"), cf(3), A.is_equal)
+    act(row(0), v("MR", 0, 128, p=(0, 1)), bias=-512.0 * 7.5, scale=-512.0)
+    M2, MS = 1.5 * 2.0 ** 36, 1.5 * 2.0 ** 18
+    for i, c_ in enumerate((M2, -M2, 127.0, 2.0 ** -18, MS, -MS, 10.0 / 32)):
+        act(row(1 + i), one1(128), scale=c_)
+    for i, c_ in enumerate((-15.5, 1.5 * 2.0 ** 28, -1.5 * 2.0 ** 28)):
+        act(row(8 + i), one1(128), scale=c_)
+    act(v("BFN"), BF, scale=-1.0)
+    ts(cf(4), cf(0), 0.5, A.add, 16384.0, A.mult)
+    ms(v("D0"), 1.0 / 32)
+    ms(v("D0", 0, D0W, 8), 512.0)
+    cp(v("PU"), v("PI"))
+    cp(v("QU"), v("QI"))
+    cp(LF, v("LI"))
+    ts(ci(1), v("THI", 0, 1), 4080, A.bitwise_and)
+    ts(ci(2), v("THI", 0, 1), 15, A.bitwise_and)
+    ts(cf(5), ci(1), -2048.0, A.mult)
+    ts(cf(11), ci(2), 0.5, A.add, -2048.0, A.mult)
+    act(v("DH"), IB, scale=cf(5))
+    act(v("DL", 0, 128), IB, scale=cf(11))
+    p8, q8 = (0, 8), (32, 40)
+    ms(v("MH"), 0.0)
+    ts(ci(3, p8), v("MGI", 0, 1, p=p8), 4080, A.bitwise_and)
+    ts(ci(4, q8), v("THI", 2, 3, p=q8), 15, A.bitwise_and)
+    ts(cf(7, p8), ci(3, p8), -512.0, A.mult)
+    ts(cf(8, q8), ci(4, q8), 0.5, A.add, -512.0, A.mult)
+    ts(v("MH", 0, 128, p=p8), v("B8", 0, 128, p=p8), 0.0, A.is_equal, cf(7, p8), A.mult)
+    ts(v("MH", 0, 128, p=q8), v("B8", 0, 128, p=q8), 0.0, A.is_equal, cf(8, q8), A.mult)
+
+    bank = [0]
+
+    def dbank():
+        bank[0] ^= 1
+        return "PD%d" % bank[0]
+
+    def window(x, col, w, eng="a", where=None):
+        b = v(where or dbank(), 0, w)
+        o = col % 256 if w <= 256 else 0
+        mm(b, [(IB, x), (v("FL", 0, 128, p=(0, 65)), v("FF", o, o + w, p=(0, 65)))])
+        c_ = 1.0 + (col - o - 2048) * E17
+        if eng == "a":
+            act(v("WW", col, col + w), b, bias=c_)
+        else:
+            ts(v("WW", col, col + w), b, c_, A.add)
+
+    tag[0] = "w"
+    for j in range(7):
+        window(v("XB", 512 * j, 512 * j + 512), 512 * j, 512, "av"[j % 2], ("PZ0", "PZ1", "PD0", "PD1")[j % 4])
+    window(v("XB", 3584, 3840), 3584, 256, "v", "PD1")
+    window(v("XB", 3840, 4096), 3840, 256, "a", "PZ0")
+    tag[0] = "i"
+    ts(v("PKB"), v("WW", 0, V), -9.0 / 32, A.add)
+    for lo, hi in ((768, 1280), (1792, 2304), (2560, 4096)):
+        dma("s", T.yx[:, lo:hi], v("XB", lo, hi), 256 * (hi - lo), after=v("WW", WN - 8, WN))
+    tt(v("DB"), v("XB", 0, K), v("XB", K, V), A.subtract)
+
+    if VUPD:
+        iota(v("FI"), [[1, 128]], 0, 0)
+        for t in range(RO - 1):
+            act(v("FR", 128 * t, 128 * t + 128), v("FI"), scale=E17, bias=-127.0 + ((1 + t % (n - 1)) * V + K * (t % 2) + CH[-1][0] - 2048) * E17)
+
+    def prepare(t, keys=False):
+        o = K * (t % 2)
+        old = (lambda a, b: v("XB", o + a, o + b)) if t < 2 else (lambda a, b: v("XS", K * (t - 2) + a, K * (t - 2) + b))
+        if keys:
+            cp(v("SU", K * t, K * t + K), v("SI", o, o + K))
+            ts(v("PM3", K, V), v("SI", o, o + K), E17, A.mult, -127.0 - 10.0 / 32 - 1.0 / 64, A.add)
+            tt(v("KO", K * t, K * t + K), v("PM3", K, V), old(0, K), A.add)
+            return
+        b = dbank()
+        for h in range(2):
+            mm(v(b, 128 * h, 128 * h + 128), [(old(128 * h, 128 * h + 128), IB)])
+        act(v("BT", K * t, K * t + K), v(b, 0, K), scale=-1.0)
+
+    prepare(0, True)
+    prepare(0)
+    prepare(1)
+    for t in range(RO):
+        c = t % 2
+        o, rv, d = K * c, K * (c ^ 1), 1 + t % (n - 1)
+        dst, src = T.cores[(rank + d) % n], T.cores[(rank - d) % n]
+        pu = v("PU", 16 * c, 16 * c + 16)
+        tag[0], tag[1] = "r" if t else "q", t
+        act(v("TF"), ind(LF, pu))
+        for h in range(2):
+            tag[0] = ("r%d" if t or h else "q%d") % h
+            mm(v("PM1", 128 * h, 128 * h + 128), [(v("PM", 256 * h + 128 * u, 256 * h + 128 * u + 128), v("TF", u, K, 2)) for u in range(2)])
+            cp(v("TU", 128 * h, 128 * h + 128), v("PM1", 128 * h, 128 * h + 128))
+        for lo, hi in GA:
+            ts(v("YA", 8 * lo, 8 * hi), ind(WW, v("TU", lo // 2, hi // 2)), -8.0 / 32, A.add)
+        for j, (lo, hi, e) in enumerate(G1):
+            tag[0] = "g%d" % j
+            src_ = ind(WW, v("SU", K * t + lo, K * t + hi))
+            if e == "a":
+                act(v("AA", 16 * lo, 16 * hi), src_, bias=127.0)
+            else:
+                ts(v("AA", 16 * lo, 16 * hi), src_, 127.0, A.add)
+        tag[0] = "h"
+        act(v("Y0"), v("YA", 7, 2048, 8), bias=127.25)
+        hp = v("PM1", K, V)
+        mm(hp, [(BP, v("Y0")), (row(0), one1(K)), (row(1), one1(K)), (row(2), one1(K)), (BN, v("Y0"))])
+        act(v("HM"), hp, FN.Relu, bias=cf(4), scale=32.0)
+        tt(v("GG"), ind(LF, v("QU", 16 * c, 16 * c + 16)), v("HM"), A.min)
+        mm(v("PM2", 0, K), [(IFN, v("TF"))], last=False)
+        mm(v("PM2", 0, K), [(BF, v("GG"))], first=False)
+        for ci_, (a, w) in enumerate(CH):
+            zb = "PZ%d" % ((ci_ + t * len(CH)) % 2)
+            end = ci_ == len(CH) - 1
+            for l0 in range(a, a + w, 32):
+                tag[0] = "b%d" % (l0 // 64)
+                b = v(dbank())
+                q = (l0 % 128, l0 % 128 + 32)
+                h0 = K * t + 128 * (l0 // 128)
+                mm(b, [(IB, v("AA", 16 * l0, 16 * l0 + 512)), (v("BT", h0, h0 + 128, p=q), v("SEL", 0, 512, p=q))])
+                act(v("AB", 16 * l0, 16 * l0 + 512), b, FN.Abs)
+                if (l0 + 32 - a) % 64 == 0:
+                    l1 = l0 - 32
+                    ec = lambda p_: v("CC", 15 - p_, 143 - p_) if p_ % 2 else v("CC", 160 - p_, 288 - p_)
+                    mm(v(zb, l1 - a, l1 - a + 64), [(v("DH"), v("ONE", 0, 64)), (v("DL", 128 * t, 128 * t + 128), v("ONE", 0, 64))]
+                       + [(ec(p_), v("AB", 16 * l1 + p_, 16 * l1 + 1024, 16)) for p_ in range(16)])
+            tag[0] = "c%d" % ci_
+            s = lambda nm, off=0: v(nm, off + a, off + a + w)
+            z, zz, kb = v(zb, 0, w), v(zb, K, K + w), s("PKB", o)
+            tt(v("YB", 8 * a, 8 * (a + w)), ind(WW, v("TU", 128 + a // 2, 128 + (a + w) // 2)), v("YA", 8 * a, 8 * (a + w)), A.min)
+            sc, yb, d0 = v("SC", 8 * a, 8 * (a + w)), v("YB", 8 * a, 8 * (a + w)), v("D0", 0, 8 * w)
+            add("v", lambda sc=sc, yb=yb, d0=d0: g.vector.tensor_tensor_scan(sc["ap"], d0["ap"], yb["ap"], 0.0, A.add, A.min), [sc], [yb, d0], 30 + CYC * 8 * w)
+            tt(s("MM"), v("SC", 8 * a + 7, 8 * (a + w), 8), kb, A.min)
+            tt(z, z, s("KO", K * t), A.max)
+            tt(s("K3"), z, s("MM"), A.min)
+            M = 1.5 * 2.0 ** 23
+            ts(s("X2"), s("K3"), M + 127, A.add, M, A.subtract)
+            pre = [(BN if c else BP, s("DB")), (v("MH", 0, 128, p=(0, 40)), v("ONE", 0, w, p=(0, 40))), (BP, s("XS", K * (t - 1)) if t else s("XB", rv))]
+            mm(zz, pre, last=False)
+            mm(zz, [(BN, s("X2"))], first=False)
+            xs = s("XS", K * t)
+            if end and FASTX:
+                tt(s("XT"), zz, s("X2"), A.max)
+                tt(xs, s("XT"), s("XB", o), A.min)
+            tt(s("KT"), zz, s("K3"), A.max)
+            tt(s("K4"), s("KT"), kb, A.min)
+            if not (end and FASTX):
+                ts(xs, s("K4"), M + 127, A.add, M, A.subtract)
+            ar = t * len(CH) + ci_
+            rid, pid, _ = topo.addr(dst)
+            land = s("LAND", K * t)
+            add("g", lambda xs=xs, land=land, ar=ar, rid=rid, pid=pid, mk=topo.mask(core, dst):
+                g.remote_dma(land["ap"], xs["ap"], T.sem["ar%d" % ar], T.sem.sent, pid, rid, mk), [], [xs], 300.0, kind="r",
+                extra=len(topo.engines(core, dst)))
+            add(None, None, [land], [], 0.0, lat=REM, kind="arr", extra=(ar, len(topo.engines(src, core)), len(ops) - 1))
+            if t == RO - 1:
+                dma("s", T.yx[:, d * V + o + a:d * V + o + a + w], land, 256 * w)
+                dma("s", T.yx[:, o + a:o + a + w], xs, 256 * w)
+            zp = s("PM3")
+            mm(zp, pre + [(IB, v("ND", t + a, t + a + w))], last=False)
+            mm(zp, [(BN, s("X2"))], first=False)
+            if end and FASTP:
+                ts(s("PT"), zp, 0.0, A.is_gt)
+                if t < RO - 1:
+                    act(s("SG"), s("PT"), acc=v("CNT", ar, ar + 1))
+            else:
+                act(s("SG"), zp, FN.Sign)
+                act(s("PT"), s("SG"), FN.Relu, acc=v("CNT", ar, ar + 1) if t < RO - 1 else None)
+            tt(s("DM"), s("PM2"), s("PT"), A.mult)
+            tt(ind(LF, v("PU", 16 * c + a // 16, 16 * c + (a + w) // 16)), s("TF"), s("DM"), A.add)
+            tag[0] = "s%d" % ci_
+            sp = z
+            c3 = 127.0 + 10.0 / 32 + 1.0 / 64
+            if MAGIC_S:
+                lev = [(IF, s("K4")), (IBN, xs)] + [(row(i), one1(w)) for i in (3, 4, 5, 6, 7)] + [(IFN, s("K4"))]
+                if t < 2 and KOACT:
+                    ko = s("KO", K * (t + 2))
+                    mm(sp, lev)
+                    act(ko, sp, scale=-1.0)
+                    mm(sp, [(IFN, ko), (IB, xs)])
+                    ts(s("SU", K * (t + 2)), sp, c3, A.subtract, -(2.0 ** 17), A.mult)
+                elif t < 2:
+                    mm(sp, lev + [(IB, xs)])
+                    ts(s("SU", K * (t + 2)), sp, c3, A.subtract, -(2.0 ** 17), A.mult)
+                    tt(s("KO", K * (t + 2)), xs, sp, A.subtract)
+                else:
+                    mm(sp, lev + [(IB, xs)])
+                    act(s("SF", o), sp, bias=c3 * 2.0 ** 17, scale=-(2.0 ** 17))
+            else:
+                ts(s("I1"), s("K4"), 2.0 ** 17, A.mult, 2048.0, A.add)
+                ts(s("I2"), s("I1"), 4095, A.bitwise_and)
+                if t < 2:
+                    cp(s("SU", K * (t + 2)), s("I2"))
+                    ts(sp, s("I2"), E17, A.mult, -c3, A.add)
+                    tt(s("KO", K * (t + 2)), sp, xs, A.add)
+                else:
+                    cp(s("SF", o), s("I2"))
+            if t == RO - 1:
+                dma("a", T.ys[:, o + a:o + a + w], s("SF", o), 512 * w)
+        if t < RO - 1:
+            a, w = CH[-1]
+            tag[0] = "u0"
+            window(v("LAND", K * t, K * t + a), d * V + o, a)
+            window(v("XS", K * t, K * t + K), o, K)
+            if t < 2:
+                prepare(t + 2)
+            tag[0] = "k"
+            if t == 0:
+                prepare(1, True)
+            tag[0] = "u1"
+            if VUPD:
+                tt(v("WW", d * V + o + a, d * V + o + K), v("LAND", K * t + a, K * t + K), v("FR", 128 * t, 128 * t + w), A.add)
+            else:
+                window(v("LAND", K * t + a, K * t + K), d * V + o + a, w)
+            tag[0] = "e"
+            dma("s", T.yx[:, d * V + o:d * V + o + K], v("LAND", K * t, K * t + K), 65536)
+            nc = (t + 1) * len(CH)
+            act(v("CJ", 0, nc), v("CNT", 0, nc), acc=cf(10))
+            mm(v("PM3", K, K + 1), [(BF, cf(10)), (row(8), one1(1)), (row(9), one1(1)), (row(10), one1(1)), (v("BFN"), cf(10))])
+            act(cf(9), v("PM3", K, K + 1), bias=cf(11), scale=2048.0)
+            act(v("DL", 128 * (t + 1), 128 * (t + 2)), IB, scale=cf(9))
+        if t == 2:
+            dma("s", T.yx[:, 0:K], v("XS", K * t, K * t + K), 65536)
+            dma("s", T.ys[:, 0:K], v("SF", 0, K), 131072)
+    dma("s", T.yl[:, 0:V], v("LF", 0, V), 262144)
+    dma("a", T.yl[:, V:NS], v("LF", V, NS), 262144)
+    return ops
+
+
+def depend(ops):
+    hist, deps = {}, []
+    for i, op in enumerate(ops):
+        dp = set()
+        for wr, regs in ((False, op["rd"]), (True, op["wr"])):
+            for nm, lo, hi in regs:
+                ps = SCRATCH[nm][0] == "psum"
+                for j, w2, l2, h2 in hist.get(nm, []):
+                    if j != i and (((wr or w2) and lo < h2 and l2 < hi) or (ps and ops[j]["eng"] != op["eng"])):
+                        dp.add(j)
+        if op["kind"] == "arr":
+            dp.add(op["x"][2])
+        for wr, regs in ((False, op["rd"]), (True, op["wr"])):
+            for nm, lo, hi in regs:
+                h = hist.setdefault(nm, [])
+                if wr and SCRATCH[nm][0] != "psum":
+                    h[:] = [e for e in h if not (lo <= e[2] and e[3] <= hi)]
+                if SCRATCH[nm][0] == "psum" and h and ops[h[-1][0]]["eng"] != op["eng"]:
+                    k = len(h)
+                    while k and ops[h[k - 1][0]]["eng"] == ops[h[-1][0]]["eng"]:
+                        k -= 1
+                    del h[:k]
+                h.append((i, wr, lo, hi))
+        deps.append(dp)
+    return deps
+
+
+def schedule(ops, deps, cost=COST, fixed=None):
+    n, LAT, BW = len(ops), cost[4], cost[6]
+    succ = [[] for _ in ops]
+    for i, dp in enumerate(deps):
+        for j in dp:
+            succ[j].append(i)
+    prio = [0.0] * n
+    for i in range(n - 1, -1, -1):
+        op = ops[i]
+        prio[i] = op["dur"] + op["lat"] + (op["x"] / BW if op["kind"] == "d" else 0) + max([prio[j] + LAT for j in succ[i]] + [0.0])
+    prio = [p + URGENT.get(op["tag"], 0.0) for p, op in zip(prio, ops)]
+    left = [len(dp) for dp in deps]
+    ready = [i for i in range(n) if not left[i]]
+    free, done, start, order, fed = {e: 0.0 for e in ("dma", "v", "a", "p", "g", "s", None)}, [0.0] * n, [0.0] * n, [], [0.0] * n
+    while ready:
+        if fixed:
+            i = fixed[len(order)]
+            s0 = max(free[ops[i]["eng"]], fed[i])
+        else:
+            st = {i: max(free[ops[i]["eng"]], fed[i]) for i in ready}
+            m = min(ready, key=lambda i: st[i] + ops[i]["dur"])
+            cand = [i for i in ready if ops[i]["eng"] == ops[m]["eng"] and st[i] <= st[m] + LOOK * ops[m]["dur"]]
+            loads = [i for i in cand if ops[i]["kind"] == "d" and not deps[i]]
+            i = min(loads) if loads else max(cand, key=lambda i: (prio[i], -i))
+            s0 = st[i]
+        op = ops[i]
+        start[i] = s0
+        if op["eng"]:
+            free[op["eng"]] = s0 + op["dur"]
+        done[i] = s0 + op["dur"] + op["lat"]
+        if op["kind"] == "d":
+            free["dma"] = done[i] = max(done[i], free["dma"]) + op["x"] / BW
+        order.append(i)
+        ready.remove(i)
+        for j in succ[i]:
+            left[j] -= 1
+            fed[j] = max(fed[j], done[i] + (0.0 if op["eng"] == "p" == ops[j]["eng"] else LAT))
+            if not left[j]:
+                ready.append(j)
+    return order, start, done
+
+
+def place(ops, deps, cost=COST, passes=6):
+    n, LAT, BW = len(ops), cost[4], cost[6]
+    succ = [[] for _ in ops]
+    for i, dp in enumerate(deps):
+        for j in dp:
+            succ[j].append(i)
+    isd = [op["kind"] == "d" for op in ops]
+    res = ["dma" if isd[i] else ops[i]["eng"] for i in range(n)]
+    dur = [ops[i]["x"] / BW if isd[i] else ops[i]["dur"] for i in range(n)]
+    pre = [ops[i]["lat"] if isd[i] else 0.0 for i in range(n)]
+    post = [0.0 if isd[i] else ops[i]["lat"] for i in range(n)]
+
+    def sweep(prio, before, after, pre, post):
+        left = [len(x) for x in before]
+        ready, fed, st, busy = [i for i in range(n) if not left[i]], [0.0] * n, [0.0] * n, {}
+        while ready:
+            i = max(ready, key=lambda i: prio[i])
+            ready.remove(i)
+            t = fed[i] + pre[i]
+            if res[i]:
+                b = busy.setdefault(res[i], [])
+                k = 0
+                while k < len(b) and b[k][0] < t + dur[i]:
+                    t = max(t, b[k][1])
+                    k += 1
+                b.insert(k, (t, t + dur[i]))
+            st[i] = t
+            for j in after[i]:
+                left[j] -= 1
+                fed[j] = max(fed[j], t + dur[i] + (0.0 if res[i] == "p" == res[j] else post[i] + LAT))
+                if not left[j]:
+                    ready.append(j)
+        return st
+
+    prio = [0.0] * n
+    for i in range(n - 1, -1, -1):
+        prio[i] = pre[i] + dur[i] + post[i] + max([prio[j] + LAT for j in succ[i]] + [0.0])
+    first = [i for i in range(n) if isd[i] and not deps[i]]
+    best = None
+    for _ in range(passes):
+        prio = [p + URGENT.get(op["tag"], 0.0) for p, op in zip(prio, ops)]
+        for i in first:
+            prio[i] = 1e9 - i
+        st = sweep(prio, deps, succ, pre, post)
+        order = sorted(range(n), key=lambda i: (-1.0, i) if i in first else (st[i] - pre[i], i))
+        span = max(schedule(ops, deps, cost, order)[2])
+        if best is None or span < best[0]:
+            best = (span, order)
+        back = sweep([st[i] + dur[i] for i in range(n)], succ, deps, post, pre)
+        prio = [back[i] + dur[i] for i in range(n)]
+    return best[1]
+
+
+def arrange(ops, deps):
+    pos = [(op["t"] * PERIOD + SLOT.get(op["tag"], 0), i) for i, op in enumerate(ops)]
+    succ = [[] for _ in ops]
+    left = [len(dp) for dp in deps]
+    for i, dp in enumerate(deps):
+        for j in dp:
+            succ[j].append(i)
+    for e in "vapgs":
+        q = sorted(p for p in pos if ops[p[1]]["eng"] == e)
+        for (_, i), (_, j) in zip(q, q[1:]):
+            succ[i].append(j)
+            left[j] += 1
+    order = [i for i in range(len(ops)) if not left[i]]
+    for i in order:
+        for j in succ[i]:
+            left[j] -= 1
+            if not left[j]:
+                order.append(j)
+    assert len(order) == len(ops)
+    return order
+
+
+def rank_program(g, core, T, topo):
+    if T.rank_of(core) is None:
+        return
+    ops = plan(g, core, T, topo)
+    deps = depend(ops)
+    order = arrange(ops, deps)
+    queue = {"v": g.vector, "a": g.scalar, "p": g.tensor, "g": g, "s": g.sync}
+    skip = lambda i, j: ops[i]["kind"] == "arr" or (ops[i]["eng"] == "p" and ops[j]["eng"] == "p")
+    needed = set(j for i, dp in enumerate(deps) for j in dp if not skip(i, j))
+    count, mark, know, seen, nd = {}, {}, {}, {e: {} for e in queue}, 0
+    for i in order:
+        op = ops[i]
+        if op["kind"] == "arr":
+            mark[i], know[i] = ("ar%d" % op["x"][0], op["x"][1]), {}
+            count[mark[i][0]] = mark[i][1]
+            continue
+        k = seen[op["eng"]]
+        for j in sorted((j for j in deps[i] if not skip(i, j)), key=lambda j: -mark[j][1]):
+            s, c = mark[j]
+            if k.get(s, 0) < c:
+                queue[op["eng"]].wait_ge(T.sem[s], c)
+                k[s] = c
+                for s2, c2 in know[j].items():
+                    k[s2] = max(k.get(s2, 0), c2)
+        if op["eng"] == "g" and op["kind"] == "c":
+            needed.add(i)
+            if k.get("sg", 0) < count.get("sg", 0):
+                g.wait_ge(T.sem.sg, count["sg"])
+                k["sg"] = count["sg"]
+        ins = op["fn"]()
+        know[i] = dict(k)
+        if op["kind"] == "r":
+            count["sent"] = count.get("sent", 0) + op["x"]
+        elif op["kind"] == "d":
+            s = "dm%d" % nd
+            nd += 1
+            ins.then_inc(T.sem[s], 16)
+            mark[i], count[s] = (s, 16), 16
+        elif i in needed:
+            s = "s" + op["eng"]
+            ins.then_inc(T.sem[s], 1)
+            count[s] = count.get(s, 0) + 1
+            mark[i] = (s, count[s])
+    for s, c in count.items():
+        g.wait_ge(T.sem[s], c)

@@ -1,71 +1,99 @@
-from concourse.bass import DstId, RemoteDMATransfer
-from concourse.mybir import dt, AluOpType, AxisListType, ActivationFunctionType
+from concourse.mybir import AluOpType, ActivationFunctionType
 
 K, V, WN, NS, RO = 256, 512, 4096, 1024, 4
-CH = [(0, 192), (192, 64)]
-G1 = [(0, 32, "a"), (32, 64, "a"), (64, 96, "a"), (96, 128, "a"), (128, 144, "a"), (144, 192, "v"), (192, 224, "a"), (224, 256, "a")]
-BASE_CH = [(0, 1024), (1024, 1024), (2048, 1024), (3072, 512), (3584, 512)]
-GA = [(0, 256)]
-MAGIC_S, FASTX, FASTP, KOACT, VUPD, LOOK = True, True, True, True, True, 0.5
+CH = [[(0, 192), (192, 64)]] * 4
+GA = [[(0, 64), (64, 128), (128, 256)]] * 4
+GB = [[(0, 128), (128, 256)]] * 4
+G1 = [[(32 * j, 32 * j + 32, False) for j in range(8)]] * 2 + [[(0, 64, False), (64, 128, False), (128, 160, False), (160, 192, True), (192, 256, True)]] * 2
+SUMS = [[(0, 128), (128, 256)]] * 2 + [[(0, 64), (64, 128), (128, 192), (192, 256)]] * 2
+LATE = [[(0, 256)], [(0, 128), (128, 128)]]
+BASE_CH = [(0, 1536), (1536, 1536), (3072, 1024)]
+FAVOR_CH = [(0, 768), (768, 1024)]
+LOADS = ["src0", "base", "grant", "favor", "th", "mg", "part", "src1", "second"]
+POOL = ["P0", "P1", "P2", "P3", "P4"]
+ORDER = {
+    "v": "*p @w WW1 BT0:0 SU0:0 WW0 PU0:q L0:0 KO0:0 AA0:0 LF0:q LF1:q CI0:q TH0:0 CF2:q TF0:0 CI1:q TU0:0 QU0:q CF0:q "
+         "@0 YA0 CF1:q YB0 YB1 SC0 GG0 MM0 X20 SC1 PT0 MM1 X21 XS0 DM0 PT1 L0:1 XS1 DM1 LF0 LF1 BT0:1 WW0 TH0:1 SU0:1 KO0:1 TU0:1 "
+         "@1 YA0 CF0:0 YB0 YB1 SC0 GG0 MM0 X20 SC1 PT0 MM1 X21 XS0 PT1 DM0 XS1 DM1 LF0 LF1 TH0:2 ZM0:0 DL0:0 K30:0 TU0:2 WW2 WW1 "
+         "@2 YA0 HH0:0 YB0 SU1:0 YB1 AA5:1 Y00 KO1:0 CF0:1 AE1 GG0 SC1 DL0:1 AE0 SC0 MM0 ZM0 K30 MM1 X20 TF0 ZM1 PT0 K31 X21 XS0 PT1 DM0 XS1 "
+         "ZM0:1 LF0 K30:1 DM1 LF1 DL0 TH0:3 HH0:1 BT0:3 TU0:3 WW1 SU1:1 "
+         "@3 YA0 ZM1:1 K31:1 HH0:2 KO1:1 HH1:1 YB0 SU2:1 Y00 YB1 AE0 SC0 KO2:1 MM0 AE1 GG0 ZM0 K30 X20 SC1 ZM1 PT0 MM1 K31 X21 DM0 XS0 PT1 LF0 XS1 "
+         "DM1 LF1 HH0 HH1 SF0 SF1",
+    "a": "*p @q EC0 WW2:w BT1:0 WW5:w WW3:w AA1:0 WW6:w WW4:w AB1:0 AB0:0 WW7:w AA2:0 "
+         "@0 YA1 YA2 Y00 CF3:q AA4 DL0:q AA3 HM0 AA5 AA6 AB5 AA7 AB2 AB4 AB3 DH0:q AB7 CJ0 AB6 WW1 WW2 "
+         "@1 YA1 YA2 Y00 AA0 BT1 AA3 AB0 HM0 AA1 BT0:2 TF0 AA2 AA4 CJ0 WW0 AB4 AB2 AB1 "
+         "@2 YA1 AB3:1 YA2 AA0 AA1 AA2 HM0 AB1 AB0 AB3 AB2 AB4 AB5 AB6 AA6:1 AB5:1 AA7:1 AB6:1 CJ0 AB7:1 CF0 WW0 WW2 "
+         "@3 YA1 YA2 AA0 AA1 AB0 AB1 AA2 AB5 AB2 AB3 AB4 HM0 AB6 TF0 SF0:2",
+}
 E17 = 2.0 ** -17
-D0W = 1536
+NCH = sum(len(c) for c in CH)
 
 SCRATCH = {
-    "XB": ("sbuf", [128, WN], "bfloat16"), "XS": ("sbuf", [128, RO * K], "bfloat16"), "LAND": ("sbuf", [128, RO * K], "bfloat16"),
+    "XB": ("sbuf", [128, WN], "bfloat16"), "X1": ("sbuf", [128, WN], "bfloat16"),
+    "XS": ("sbuf", [128, RO * K], "bfloat16"), "LAND": ("sbuf", [128, RO * K], "bfloat16"),
     "WW": ("sbuf", [128, WN], "float32"), "LI": ("sbuf", [128, NS], "int32"), "LF": ("sbuf", [128, NS], "float32"),
     "SI": ("sbuf", [128, V], "int32"), "SU": ("sbuf", [128, RO * K], "uint16"), "SF": ("sbuf", [128, V], "float32"),
     "PI": ("sbuf", [128, 32], "int32"), "QI": ("sbuf", [128, 32], "int32"), "PU": ("sbuf", [128, 32], "uint16"), "QU": ("sbuf", [128, 32], "uint16"),
-    "AA": ("sbuf", [128, WN], "bfloat16"), "AB": ("sbuf", [128, WN], "bfloat16"),
+    "AA": ("sbuf", [128, RO * WN], "bfloat16"), "AB": ("sbuf", [128, RO * WN], "bfloat16"),
     "YA": ("sbuf", [128, 2048], "float32"), "YB": ("sbuf", [128, 2048], "float32"), "SC": ("sbuf", [128, 2048], "float32"),
-    "D0": ("sbuf", [128, D0W], "bfloat16"), "TF": ("sbuf", [128, K], "float32"),
-    "TU": ("sbuf", [128, K], "uint16"), "KO": ("sbuf", [128, RO * K], "float32"), "MM": ("sbuf", [128, K], "float32"),
-    "K3": ("sbuf", [128, K], "float32"), "K4": ("sbuf", [128, K], "float32"), "KT": ("sbuf", [128, K], "float32"), "X2": ("sbuf", [128, K], "bfloat16"),
-    "Y0": ("sbuf", [128, K], "bfloat16"), "HM": ("sbuf", [128, K], "float32"), "GG": ("sbuf", [128, K], "float32"),
-    "SG": ("sbuf", [128, K], "float32"), "PT": ("sbuf", [128, K], "float32"), "DM": ("sbuf", [128, K], "float32"),
-    "I1": ("sbuf", [128, K], "int32"), "I2": ("sbuf", [128, K], "int32"),
-    "BT": ("sbuf", [128, RO * K], "bfloat16"), "CNT": ("sbuf", [128, 16], "float32"),
+    "D0": ("sbuf", [128, 8 * max(w for c in CH for _, w in c)], "bfloat16"), "TF": ("sbuf", [128, K], "float32"), "TU": ("sbuf", [128, K], "uint16"),
+    "KO": ("sbuf", [128, RO * K], "float32"), "MM": ("sbuf", [128, RO * K], "float32"), "K3": ("sbuf", [128, RO * K], "float32"),
+    "HH": ("sbuf", [128, RO * K], "float32"), "PT": ("sbuf", [128, RO * K], "bfloat16"), "X2": ("sbuf", [128, K], "bfloat16"),
+    "Y0": ("sbuf", [128, K], "bfloat16"), "HM": ("sbuf", [128, K], "float32"), "GG": ("sbuf", [128, K], "float32"), "DM": ("sbuf", [128, K], "float32"),
+    "EC": ("sbuf", [128, V], "float32"), "CNT": ("sbuf", [128, 16], "float32"), "CJ": ("sbuf", [128, K], "bfloat16"),
     "KJ": ("sbuf", [128, 260], "int32"), "KA": ("sbuf", [128, 260], "int32"), "ND": ("sbuf", [128, 260], "bfloat16"),
-    "BK": ("sbuf", [128, 128], "int32"), "MR": ("sbuf", [128, 128], "float32"), "SB": ("sbuf", [128, 128], "float32"), "SB2": ("sbuf", [128, 128], "float32"),
-    "SLI": ("sbuf", [128, 512], "int32"), "SEL": ("sbuf", [128, 512], "bfloat16"), "B8": ("sbuf", [128, 128], "int32"),
+    "MR": ("sbuf", [128, 128], "float32"), "SB": ("sbuf", [128, 128], "float32"), "SB2": ("sbuf", [128, 128], "float32"),
+    "ZF": ("sbuf", [128, 128], "float32"), "E8": ("sbuf", [128, 128], "float32"),
     "IB": ("sbuf", [128, 128], "bfloat16"), "IBN": ("sbuf", [128, 128], "bfloat16"), "IF": ("sbuf", [128, 128], "float32"), "IFN": ("sbuf", [128, 128], "float32"),
-    "BP": ("sbuf", [128, 128], "bfloat16"), "BN": ("sbuf", [128, 128], "bfloat16"), "BF": ("sbuf", [128, 128], "float32"),
-    "CC": ("sbuf", [128, 288], "bfloat16"), "PM": ("sbuf", [128, 512], "float32"), "FF": ("sbuf", [128, 512], "bfloat16"), "FL": ("sbuf", [128, 128], "bfloat16"),
-    "ONE": ("sbuf", [128, K], "bfloat16"), "RW": ("sbuf", [128, 11 * 128], "bfloat16"),
+    "BP": ("sbuf", [128, 128], "bfloat16"), "BN": ("sbuf", [128, 128], "bfloat16"), "BF": ("sbuf", [128, 128], "float32"), "BFN": ("sbuf", [128, 128], "float32"),
+    "CC": ("sbuf", [128, 288], "bfloat16"), "PM": ("sbuf", [128, 512], "float16"), "FF": ("sbuf", [128, 512], "bfloat16"), "FL": ("sbuf", [128, 384], "bfloat16"),
+    "ONE": ("sbuf", [128, K], "bfloat16"), "RW": ("sbuf", [128, 9 * 128], "bfloat16"),
+    "TH": ("sbuf", [128, K], "float16"), "IH": ("sbuf", [128, 128], "float16"), "LV": ("sbuf", [128, K], "bfloat16"),
     "THI": ("sbuf", [128, 4], "int32"), "MGI": ("sbuf", [128, 4], "int32"), "CI": ("sbuf", [128, 16], "int32"), "CF": ("sbuf", [128, 16], "float32"),
-    "DH": ("sbuf", [128, 128], "bfloat16"), "DL": ("sbuf", [128, RO * 128], "bfloat16"), "MH": ("sbuf", [128, 128], "bfloat16"), "DB": ("sbuf", [128, K], "bfloat16"),
-    "FI": ("sbuf", [128, 128], "float32"), "FR": ("sbuf", [128, 384], "float32"), "BFN": ("sbuf", [128, 128], "float32"), "XT": ("sbuf", [128, K], "bfloat16"), "CJ": ("sbuf", [128, 16], "float32"),
+    "BT": ("sbuf", [128, RO * K], "bfloat16"), "SLI": ("sbuf", [128, V], "int32"), "SEL": ("sbuf", [128, V], "bfloat16"),
+    "BR": ("sbuf", [128, WN], "bfloat16"), "AE": ("sbuf", [128, 2048], "float32"),
+    "DH": ("sbuf", [128, 128], "bfloat16"), "DL": ("sbuf", [128, RO * 128], "bfloat16"),
 }
-for _b in ("PD0", "PD1", "PZ0", "PZ1", "PKB", "PM1", "PM2", "PM3"):
+for _b in POOL + ["PZ0", "PZ1", "PS"]:
     SCRATCH[_b] = ("psum", [128, 512], "float32")
 NDMA = 40
-SEMAPHORES = ["sv", "sa", "sp", "sg", "sent"] + ["dm%d" % i for i in range(NDMA)] + ["ar%d" % i for i in range(RO * len(CH))]
+SEMAPHORES = ["sv", "sa", "sp", "sg", "sent"] + ["dm%d" % i for i in range(NDMA)] + ["ar%d" % i for i in range(NCH)]
 ESZ = {"bfloat16": 2, "float16": 2, "uint16": 2, "float32": 4, "int32": 4}
 A = AluOpType
 FN = ActivationFunctionType
-COST = (1.0, 0.5, 1.56, 3.8, 90.0, 2600.0, 200.0)
-PERIOD = 1700
-SLOT = {k: int(x) for k, x in (y.split("=") for y in """
-PI:ia=-3000 LI:ia=-2999 SI:ia=-2998 XB:ia=-2997 XB:ib=-2996 XB:ic=-2995 XB:id=-2994 XB:ie=-2993 THI:ia=-2992 MGI:ia=-2991 THI:ib=-2990 QI:ia=-2989 SI:ib=-2988 ONE:ia=-2227 FL:ia=-2105 CC:ia=-2105 FF:ia=-2095 FL:ib=-2094 D0:ia=-2007 KA:ia=-1991 CI:ia=-1987 CF:ia=-1908 ND:ia=-1907 FF:ic=-1886 BF:ia=-1845 FL:ic=-1826 CF:ib=-1690 CF:id=-1626 RW:ic=-1467 MH:ia=-1448 PU:ia=-1392 FL:id=-1391 CF:ic=-1391 D0:ib=-1390 IB:ia=-1378 RW:ib=-1308 SB2:ia=-1270 FF:id=-1119 SB:ia=-1108 CF:ie=-999 PM:id=-971 PM:ic=-932 RW:ie=-929 RW:ij=-918 PM:ib=-914 PM:ia=-913 SU:ia=-913 PM3:ia=-912 LF:ia=-911 KO:ia=-911 PD:ia=-910 DB:ia=-910 WW:ib=-909 PKB:ia=-909 WW:id=-908 WW:if=-907 CI:ib=-906 CI:id=-897 CF:if=-875 CI:ie=-875 CI:ic=-874 CF:ih=-874 CF:ii=-874 MH:ib=-873 WW:ih=-872 QU:ia=-861 RW:ik=-840 FR:ia=-839 RW:id=-838 FR:ic=-838 FR:ib=-837 CC:ic=-817 MH:ic=-800 PD:ib=-769 PD:ic=-768 CF:ig=-742 PD:id=-717 CC:ib=-622 RW:ii=-610 FI:ia=-607 KJ:ia=-606 FF:ib=-594 BP:ia=-569 BN:ia=-569 RW:ia=-569 BFN:ia=-569 IBN:ia=-558 IF:ia=-548 WW:ia=-537 PD:ie=-520 TF:ra=-516 RW:ig=-207 WW:ic=-206 BK:ia=-172 B8:ia=-161 MR:ia=-140 B8:ib=-139 SLI:ia=-88 AA:g5a=-35 RW:ih=35 IFN:ia=36 WW:ie=36 PD:if=81 PD:ig=81 PD:ih=91 PM1:r0a=92 DH:ia=213 AA:g0a=224 WW:ig=224 DL:ia=236 BT:ib=236 BT:ia=237 AA:g1a=238 AA:g2a=238 AB:b0a=238 AB:b0b=239 AA:g3a=240 PD:ii=312 PD:ij=313 PD:ik=331 PD:il=332 PM3:c0a=333 PM2:ha=334 PD:b0a=334 PM1:r1a=335 PD:b0b=336 PD:b1a=367 AA:g4a=519 Y0:ha=528 AB:b1a=528 out:c0a=531 AB:b1b=548 PZ:b0a=628 AA:g6a=629 AB:b2a=630 PD:b1b=695 AB:b2b=750 AA:g7a=801 PM1:ha=816 out:c1a=862 TU:r0a=1031 PD:b2a=1086 PD:b2b=1090 PZ:b1a=1111 PD:b3a=1112 AB:b3a=1138 AB:b3b=1138 RW:if=1138 HM:ha=1139 SG:c0a=1139 PT:c0a=1139 SG:c1a=1139 CJ:ea=1141 SF:s0a=1142 out:s0a=1142 KO:s0a=1142 WW:u0b=1143 CF:ea=1143 DL:ea=1143 KO:s1a=1144 SF:s1a=1145 out:s1a=1156 out:s1c=1157 SEL:ia=1162 YA:r1a=1163 PZ:b2a=1163 PD:b3b=1163 PZ:c0b=1164 PZ:b3a=1165 PZ:c0c=1166 PM3:c0b=1166 PM2:hb=1167 PZ:c1b=1168 PZ:c1c=1168 PM3:c1a=1168 PM3:c1b=1179 PZ:s0a=1180 TU:r1a=1184 YB:c0a=1184 YB:c1a=1184 SC:c0a=1185 PZ:c0a=1185 MM:c0a=1186 K3:c0a=1186 SC:c1a=1186 X2:c0a=1187 MM:c1a=1188 GG:ha=1189 PZ:c1a=1189 KT:c0a=1190 K3:c1a=1190 K4:c0a=1191 out:ia=1193 PD:u0b=1197 X2:c1a=1202 out:ib=1202 PM3:ea=1218 PZ:s1a=1239 PZ:s0b=1240 PZ:s1b=1251 PD:u0a=1252 PD:u0c=1253 out:eb=1261 XS:c0a=1262 XT:c1a=1262 KT:c1a=1263 XS:c1a=1273 PT:c1a=1273 K4:c1a=1274 PM3:ka=1274 DM:c0a=1280 DM:c1a=1280 KO:ka=1281 SU:ka=1282 LF:c0a=1283 LF:c1a=1286 SU:s0a=1287 SU:s1a=1298 WW:u1a=1299 out:c0c=1342 out:ic=1343 out:c1c=1363 out:s1b=1363 out:ec=1364 out:ea=1384 PD:u0d=1543 out:c1b=1564 out:c0b=1565 WW:u0a=1566 BT:u0a=1931
-ONE:ia=-1841 FL:ia=-1840 MH:ia=-1679 FL:ib=-1549 D0:ia=-1458 KA:ia=-1426 CI:ia=-1406 CF:ia=-1405 FL:ic=-1404 CF:ic=-1403 CF:id=-1350 IB:ia=-1349 PU:ia=-1348 FF:ia=-1336 BF:ia=-1336 CC:ia=-1335 CF:ib=-1324 CF:ie=-1315 SB2:ia=-1314 FL:id=-1312 SB:ia=-1311 D0:ib=-1310 PM:ib=-1309 PM:ia=-1281 PM:id=-1210 FF:ic=-1209 PM:ic=-1208 FF:id=-1133 ND:ia=-932 PM3:ia=-932 LF:ia=-932 SU:ia=-931 KO:ia=-931 DB:ia=-930 SEL:ia=-929 PKB:ia=-928 TU:q0a=-928 WW:wb=-927 WW:wd=-926 CI:ib=-925 CI:id=-905 CI:ie=-905 CF:if=-904 CF:ih=-904 WW:wf=-904 WW:wh=-904 CI:ic=-903 CF:ii=-902 RW:ij=-888 QU:ia=-872 MH:ib=-721 RW:ih=-668 RW:ie=-667 RW:ig=-653 RW:ic=-652 FR:ia=-624 RW:ii=-623 FR:ib=-594 FR:ic=-589 RW:ik=-588 RW:ib=-587 RW:id=-586 IFN:ia=-583 IBN:ia=-582 TF:ra=-539 CC:ic=-501 CC:ib=-480 IF:ia=-441 BP:ia=-440 FI:ia=-213 KJ:ia=17 BK:ia=18 B8:ia=47 BFN:ia=119 BN:ia=128 RW:ia=128 TF:qa=129 WW:wa=130 WW:wc=130 WW:we=131 WW:wg=131 DH:ia=132 BT:ib=132 WW:wi=132 AA:g0a=162 BT:ia=163 DL:ia=202 AA:g1a=203 PZ:wa=237 PM1:r0a=238 AB:b0a=243 MR:ia=257 PM1:q0a=267 PZ:wb=268 PD:wa=268 B8:ib=279 PD:wb=310 PZ:wc=310 PD:wc=310 FF:ib=311 PZ:wd=311 PZ:we=311 PD:ic=312 PD:id=312 PM2:ha=312 PD:wd=312 PD:ia=313 PD:ib=313 PM3:c0a=314 PD:b0a=314 PM1:r1a=314 SLI:ia=322 out:c0a=322 out:c1a=323 PD:b0b=325 AA:g2a=359 AB:b0b=359 Y0:ha=360 PD:b1a=366 PZ:b0a=394 AA:g3a=401 AA:g4a=409 AB:b1a=410 AB:b1b=471 PM1:ha=495 AA:g6a=620 AB:b2a=720 PD:b1b=728 AB:b2b=741 AA:g7a=810 TU:r0a=812 AB:b3a=831 PD:b2a=908 PD:b2b=909 PZ:b1a=911 PD:b3a=911 PZ:b2a=952 CF:ig=1041 MH:ic=1042 out:c0c=1048 out:c1c=1049 AB:b3b=1077 YA:r1a=1122 HM:ha=1138 RW:if=1139 SG:c0a=1139 PT:c0a=1139 SG:c1a=1139 CJ:ea=1139 SF:s0a=1140 KO:s0a=1141 WW:u0b=1141 CF:ea=1141 DL:ea=1141 out:s0a=1142 KO:s1a=1142 PD:b3b=1154 out:eb=1156 PZ:c0b=1165 PZ:b3a=1165 out:ib=1165 PZ:c0c=1166 PM3:c0b=1166 out:ia=1166 PM2:hb=1167 PZ:c1b=1168 PZ:c1c=1168 PM3:c1a=1168 PM3:c1b=1168 PZ:s0a=1169 PD:u0b=1169 PM3:ea=1169 PZ:s1a=1170 SF:s1a=1175 PZ:s0b=1181 TU:r1a=1183 AA:g5a=1184 YB:c0a=1184 YB:c1a=1184 SC:c0a=1185 PZ:c0a=1185 MM:c0a=1186 K3:c0a=1186 SC:c1a=1186 X2:c0a=1187 MM:c1a=1187 out:s1b=1196 GG:ha=1198 out:ic=1209 out:ea=1210 out:ec=1211 out:s1a=1215 out:s1c=1216 PZ:c1a=1249 WW:u0a=1256 PZ:s1b=1261 KT:c0a=1274 K3:c1a=1274 K4:c0a=1275 X2:c1a=1275 XS:c0a=1276 XT:c1a=1276 KT:c1a=1276 XS:c1a=1277 PT:c1a=1277 out:c1b=1277 K4:c1a=1278 PM3:ka=1280 DM:c0a=1280 DM:c1a=1281 KO:ka=1281 SU:ka=1282 LF:c0a=1282 LF:c1a=1282 SU:s0a=1283 SU:s1a=1284 WW:u1a=1284 PD:u0a=1322 out:c0b=1329 BT:u0a=1881 PD:u0c=1968 PD:u0d=1969
-""".split())}
-URGENT = {}
+CYC, PEC, GAT, SCA, WAKE, REM, DLAT, BW = 1.0, 0.5, 1.56, 3.8, 100.0, 2200.0, 1400.0, 220.0
+ROWS = 50000
+LOOK, AHEAD, STEP, PASSES = 400.0, 3, 3, 2
+KEPT = {}
 
 
-def plan(g, core, T, topo, cost=COST):
+def plan(g, core, T, topo, bank):
     rank, n = T.rank_of(core), len(T.cores)
-    CYC, PEC, GAT, SCA, _, REM, _ = cost
-    ops, tag, seen = [], ["i", 0], {}
+    ops, leases, now, seen = [], [0], ["p"], {}
 
     def v(name, lo=None, hi=None, step=1, p=(0, 128)):
+        where, shape, kind = SCRATCH.get(name, SCRATCH["P0"])
         if lo is None:
-            lo, hi = 0, SCRATCH[name][1][1]
-        ap = T[name][p[0]:p[1], lo:hi:step] if step != 1 else T[name][p[0]:p[1], lo:hi]
-        return {"ap": ap, "reg": [(name, lo, hi)], "n": len(range(lo, hi, step)), "sz": ESZ[SCRATCH[name][2]], "ps": SCRATCH[name][0] == "psum"}
+            lo, hi = 0, shape[1]
+        return {"at": (name, p, lo, hi, step), "reg": [(name, lo, hi) + p], "n": len(range(lo, hi, step)), "sz": ESZ[kind], "ps": where == "psum"}
+
+    def lease():
+        leases[0] += 1
+        return "lease%d" % leases[0]
 
     def ind(win, off):
-        return {"ap": win["ap"].indirect(off["ap"]), "reg": win["reg"], "off": off["reg"], "n": 16 * off["n"], "sz": 4, "ps": False, "ind": True}
+        return {"win": win, "idx": off, "reg": win["reg"], "off": off["reg"], "n": 16 * off["n"], "sz": 4, "ps": False}
 
-    def add(eng, fn, outs, ins, dur, lat=0.0, kind="c", extra=None):
+    def a_(x):
+        if not isinstance(x, dict):
+            return x
+        if "win" in x:
+            return a_(x["win"]).indirect(a_(x["idx"]))
+        name, p, lo, hi, step = x["at"]
+        t_ = T[bank.get(name, name)]
+        return t_[p[0]:p[1], lo:hi:step] if step != 1 else t_[p[0]:p[1], lo:hi]
+
+    def add(ways, outs, ins, lat=0.0, kind="c", extra=None):
         rd, wr = [], []
         for x in ins:
             if isinstance(x, dict):
@@ -73,111 +101,135 @@ def plan(g, core, T, topo, cost=COST):
         for x in outs:
             wr += x["reg"]
             rd += x.get("off", [])
-        ops.append({"eng": eng, "fn": fn, "rd": rd, "wr": wr, "dur": dur, "lat": lat, "kind": kind, "x": extra,
-                    "t": tag[1]})
-        key = "%s:%s" % (wr[0][0].rstrip("01") if wr and wr[0][0][:2] in ("PD", "PZ") else wr[0][0] if wr else "out", tag[0])
-        seen[key, tag[1]] = seen.get((key, tag[1]), -1) + 1
-        ops[-1]["tag"] = "%s%s" % (key, "abcdefghijklmnopqrstuvwxyz"[seen[key, tag[1]]])
-
-    def a_(x):
-        return x["ap"] if isinstance(x, dict) else x
+        ops.append({"ways": ways, "rd": rd, "wr": wr, "lat": lat, "kind": kind, "x": extra, "tag": None})
+        if "v" in ways or "a" in ways:
+            nm = wr[0][0]
+            nm = "L" if nm[:5] == "lease" else "ZM" if nm[:2] == "PZ" else "XS" if nm == "X1" else nm
+            seen[nm, now[0]] = seen.get((nm, now[0]), -1) + 1
+            ops[-1]["tag"] = "%s%d:%s" % (nm, seen[nm, now[0]], now[0])
 
     def vcost(out, x, two=1.0):
-        if out.get("ind"):
+        if "win" in out:
             return 50 + SCA * CYC * out["n"]
-        if x.get("ind"):
+        if "win" in x:
             return 50 + GAT * CYC * x["n"]
         return 30 + CYC * max(64, x["n"] * two * (0.5 if out["sz"] == 2 and x["sz"] == 2 and two == 1.0 else 1))
 
-    def ts(out, x, s1, op0, s2=None, op1=None):
+    def ts_(out, x, s1, op0, s2=None, op1=None):
         if op1 is None:
-            fn = lambda: g.vector.tensor_scalar(out["ap"], x["ap"], a_(s1), None, op0)
-        else:
-            fn = lambda: g.vector.tensor_scalar(out["ap"], x["ap"], a_(s1), a_(s2), op0, op1)
-        add("v", fn, [out], [x, s1, s2], vcost(out, x))
+            return lambda: g.vector.tensor_scalar(a_(out), a_(x), a_(s1), None, op0), vcost(out, x)
+        return lambda: g.vector.tensor_scalar(a_(out), a_(x), a_(s1), a_(s2), op0, op1), vcost(out, x)
 
-    def tt(out, x, y, op):
-        add("v", lambda: g.vector.tensor_tensor(out["ap"], x["ap"], y["ap"], op), [out], [x, y], vcost(out, x, 1.0001 if x["ps"] or y["ps"] else 2.0))
+    def act_(out, x, func=FN.Identity, bias=0.0, scale=1.0, acc=None):
+        cost = 60 + CYC * max(64, x["n"] * (GAT if "win" in x else 1))
+        if acc is None:
+            return lambda: g.scalar.activation(a_(out), a_(x), func, bias=a_(bias), scale=a_(scale)), cost
+        return lambda: g.scalar.activation(a_(out), a_(x), func, bias=a_(bias), scale=a_(scale), accum_out=a_(acc)), cost + 20
 
-    def cp(out, x):
-        add("v", lambda: g.vector.tensor_copy(out["ap"], x["ap"]), [out], [x], vcost(out, x))
-
-    def ms(out, c):
-        add("v", lambda: g.vector.memset(out["ap"], c), [out], [], vcost(out, out))
+    def ts(out, x, s1, op0, s2=None, op1=None):
+        add({"v": ts_(out, x, s1, op0, s2, op1)}, [out], [x, s1, s2])
 
     def act(out, x, func=FN.Identity, bias=0.0, scale=1.0, acc=None):
-        if acc is None:
-            fn = lambda: g.scalar.activation(out["ap"], x["ap"], func, bias=a_(bias), scale=a_(scale))
-        else:
-            fn = lambda: g.scalar.activation(out["ap"], x["ap"], func, bias=a_(bias), scale=a_(scale), accum_out=acc["ap"])
-        add("a", fn, [out] + ([acc] if acc else []), [x, bias, scale], 65 + CYC * max(64, x["n"] * (GAT if x.get("ind") else 1)))
+        add({"a": act_(out, x, func, bias, scale, acc)}, [out] + ([acc] if acc else []), [x, bias, scale])
 
-    def mm(out, terms, first=True, last=True):
+    def lin(out, x, scale=1.0, bias=0.0):
+        add({"a": act_(out, x, bias=bias, scale=scale), "v": ts_(out, x, scale, A.mult, bias, A.add)}, [out], [x, scale, bias])
+
+    def tt(out, x, y, op):
+        add({"v": (lambda: g.vector.tensor_tensor(a_(out), a_(x), a_(y), op), vcost(out, x, 1.0001 if x["ps"] or y["ps"] else 2.0))}, [out], [x, y])
+
+    def cp(out, x):
+        add({"v": (lambda: g.vector.tensor_copy(a_(out), a_(x)), vcost(out, x))}, [out], [x])
+
+    def ms(out, c):
+        add({"v": (lambda: g.vector.memset(a_(out), c), vcost(out, out))}, [out], [])
+
+    def mm(out, terms, first=True, last=True, hot=False):
         def fn():
             r = None
             for i, (l, x) in enumerate(terms):
-                r = g.tensor.matmul(out["ap"], l["ap"], x["ap"], first and i == 0, last and i == len(terms) - 1)
+                r = g.tensor.matmul(a_(out), a_(l), a_(x), first and i == 0, last and i == len(terms) - 1)
             return r
-        o = out if first and last else {"reg": [(out["reg"][0][0], 0, 512)]}
-        add("p", fn, [o], [y for t_ in terms for y in t_], sum(PEC * max(64, x["n"]) * (4 if x["sz"] == 4 else 1) for _, x in terms), lat=60.0,
-            kind="c" if first else "acc")
+        add({"p": (fn, sum(PEC * max(64, x["n"]) * (4 if x["sz"] == 4 else 1) for _, x in terms))}, [out], [y for t_ in terms for y in t_], lat=60.0)
+        ops[-1]["hot"] = hot
 
     def iota(out, pat, base, cm):
         if SCRATCH[out["reg"][0][0]][2] == "int32":
-            fn = lambda: g.iota(out["ap"], pat, base, cm)
+            fn = lambda: g.iota(a_(out), pat, base, cm)
         else:
-            fn = lambda: g.iota(out["ap"], pat, base, cm, allow_small_or_imprecise_dtypes=True)
-        add("g", fn, [out], [], 130 + 2 * CYC * out["n"])
+            fn = lambda: g.iota(a_(out), pat, base, cm, allow_small_or_imprecise_dtypes=True)
+        add({"g": (fn, 130 + 2 * CYC * out["n"])}, [out], [])
 
-    def dma(q, out, x, nbytes, after=None):
-        e = g.sync if q == "s" else g.scalar
-        add(q, lambda: e.dma_start(a_(out), a_(x)), [out] if isinstance(out, dict) else [], [x, after], 60.0, lat=1800.0, kind="d", extra=nbytes)
+    def dma(out, x, nbytes, after=None):
+        add({"s": (lambda: g.sync.dma_start(a_(out), a_(x)), 60.0)}, [out] if isinstance(out, dict) else [], [x, after], kind="d", extra=nbytes + ROWS)
 
     row = lambda i: v("RW", 128 * i, 128 * i + 128, p=(0, 1))
-    one1 = lambda w: v("ONE", 0, w, p=(0, 1))
+    one = lambda w, k=1: v("ONE", 0, w, p=(0, k))
+    fl = lambda j, k: v("FL", 128 * j, 128 * j + 128, p=(0, k))
     cf = lambda i, p=(0, 128): v("CF", i, i + 1, p=p)
     ci = lambda i, p=(0, 128): v("CI", i, i + 1, p=p)
     IB, IBN, IF, IFN, BP, BN, BF = (v(x) for x in ("IB", "IBN", "IF", "IFN", "BP", "BN", "BF"))
     WW, LF = v("WW"), v("LF")
+    p8 = (0, 8)
+    xs_ = lambda t, a, b: v("X1", a, b) if t == 0 else v("XS", K * t + a, K * t + b)
+    land_ = lambda t, a, b: v("X1", V + a, V + b) if t == 0 else v("LAND", K * t + a, K * t + b)
 
-    dma("s", v("PI"), T.grant[:], 16384)
-    dma("s", v("LI"), T.favor[:], 524288)
-    dma("s", v("SI", 0, K), T.src[:, 0:K], 131072)
-    for j, (lo, w) in enumerate(BASE_CH):
-        dma("s", v("XB", lo, lo + w), T.base[:, lo:lo + w], 256 * w)
-    dma("s", v("THI", 0, 1), T.th[:], 8192)
-    dma("s", v("MGI", 0, 1, p=(0, 8)), T.mg[:], 512)
-    dma("s", v("THI", 2, 3, p=(32, 40)), T.mg[:], 512)
-    dma("s", v("QI"), T.part[:], 16384)
-    dma("s", v("SI", K, V), T.src[:, K:V], 131072)
+    loads = {
+        "src0": [(v("SI", 0, K), T.src[:, 0:K], 131072)], "src1": [(v("SI", K, V), T.src[:, K:V], 131072)],
+        "base": [(v("XB", lo, lo + w), T.base[:, lo:lo + w], 256 * w) for lo, w in BASE_CH],
+        "grant": [(v("PI"), T.grant[:], 16384)], "part": [(v("QI"), T.part[:], 16384)], "favor": [(v("LI", lo, hi), T.favor[:, lo:hi], 512 * (hi - lo)) for lo, hi in FAVOR_CH],
+        "th": [(v("THI", 0, 1), T.th[:], 8192)], "mg": [(v("MGI", 0, 1, p=p8), T.mg[:], 512)],
+        "second": [(v("X1", lo, hi), T.base[:, lo:hi], 256 * (hi - lo)) for lo, hi in ((K, V), (V + K, WN))],
+    }
+    for name in LOADS:
+        for out, x, nb in loads[name]:
+            dma(out, x, nb)
+
+    M2, MS, MA, M = 1.5 * 2.0 ** 36, 1.5 * 2.0 ** 18, 1.5 * 2.0 ** 28, 1.5 * 2.0 ** 23
+    ms(v("FF"), 1.0)
+    ms(v("FL"), 0.0)
+    ms(v("ONE"), 1.0)
+    ms(v("ZF"), 0.0)
+    ms(v("FF", 0, 256, p=(64, 65)), 0.0)
+    ms(v("CC"), 0.0)
+    zb, zf, blocks = v("FL", 256, 384), v("ZF"), [[-16, 8], [0, 16]]
+
+    def pick(out, x, pat, op, c_, base=0, cm=1):
+        add({"g": (lambda: g.affine_select(a_(out), a_(x), pat, op, c_, base, cm), 170 + 2 * CYC * out["n"])}, [out], [x])
+
+    def band(out, x, c_):
+        pick(out, x, blocks, A.is_ge, c_, -16)
+        pick(out, out, blocks, A.is_ge, 0.0)
 
     iota(v("KJ"), [[-1, 260]], 1024, 1)
-    iota(v("BK"), [[-16, 8], [0, 16]], 0, 1)
-    iota(v("MR"), [[0, 8], [1, 16]], 0, 0)
-    ms(v("FF"), 0.0)
     iota(v("FF", 0, 512, p=(0, 1)), [[0, 2], [1, 256]], 0, 0)
+    band(BF, zf, 1.0)
+    iota(v("MR"), [[0, 8], [1, 16]], 0, 0)
     iota(v("SLI"), [[-1, 32], [0, 16]], 0, 1)
-    iota(v("B8", 0, 128, p=(0, 8)), [[-1, 8], [0, 16]], 0, 1)
-    iota(v("B8", 0, 128, p=(32, 40)), [[-1, 8], [0, 16]], 0, 1)
-    ms(v("FF", 0, 512, p=(32, 33)), 1.0)
-    ms(v("FF", 256, 512, p=(64, 65)), 1.0)
-    ms(v("FL"), 0.0)
-    for pp, c_ in ((0, E17), (32, -128.0), (64, 2.0 ** -9)):
-        ms(v("FL", 0, 128, p=(pp, pp + 1)), c_)
-    ms(v("ONE"), 1.0)
+    pick(v("E8", 0, 128, p=p8), v("ZF", 0, 128, p=p8), [[-1, 8], [0, 16]], A.not_equal, 1.0)
+    band(BP, zb, 512.0)
+    band(BN, zb, -512.0)
+    for i, c_ in enumerate((M2, -M2, -2048.0, MS, -15.5, MA, -MA)):
+        pick(row(1 + i), one(128), [[0, 128]], A.is_gt, c_, 0, 0)
+    band(v("BFN"), zf, -1.0)
+    for out, x, c_ in ((IBN, zb, -1.0), (IF, zf, 1.0), (IFN, zf, -1.0)):
+        pick(out, x, [[-1, 128]], A.not_equal, c_)
+    for j, rows in enumerate(((E17, -128.0, 2.0 ** -9, 45.0 / 64), (127.0, 11.0 / 32), (-MS, 127.0, 10.0 / 32))):
+        for i, c_ in enumerate(rows):
+            out, x = v("FL", 128 * j, 128 * j + 128, p=(32 * i, 32 * i + 1)), v("ONE", 0, 128, p=(32 * i, 32 * i + 1))
+            if j:
+                pick(out, x, [[0, 128]], A.is_gt, c_, 0, 0)
+            else:
+                act(out, x, scale=c_)
     ts(IB, v("KJ", 0, 128), 1024.0, A.is_equal)
-    act(IBN, IB, scale=-1.0)
-    act(IF, IB)
-    act(IFN, IB, scale=-1.0)
     ts(v("KA"), v("KJ"), 15, A.bitwise_and)
     cp(cf(0), v("KA", 0, 1))
+    ms(v("D0"), 1.0 / 32)
+    ms(v("D0", 0, SCRATCH["D0"][1][1], 8), 512.0)
     ts(v("ND"), v("KA"), 0.0, A.not_equal, -(2.0 ** 23), A.mult)
-    ts(BF, v("BK"), cf(0), A.is_equal)
-    act(BP, BF, scale=512.0)
-    act(BN, BF, scale=-512.0)
-    ms(v("CC"), 0.0)
     act(v("CC", 15, 143, 16), v("BF", 0, 128, 16), scale=2048.0)
     act(v("CC", 160, 288, 16), v("BF", 0, 128, 16), scale=2048.0)
+    act(row(0), v("MR", 0, 128, p=(0, 1)), bias=-512.0 * 7.5, scale=-512.0)
     ts(v("SB2"), v("MR"), cf(0), A.add, 1.0, A.add)
     tt(v("SB"), v("SB2"), BF, A.mult)
     ts(cf(1), cf(0), 8.0, A.is_lt)
@@ -186,228 +238,212 @@ def plan(g, core, T, topo, cost=COST):
     ts(v("PM", 128, 256), v("SB"), 16.0, A.is_equal, cf(1), A.mult)
     ts(v("PM", 256, 384), v("SB"), 16.0, A.is_equal, cf(2), A.mult)
     ts(v("PM", 384, 512), v("SB"), 24.0, A.is_equal)
+    ts(v("IH"), v("KJ", 0, 128), 1024.0, A.is_equal, -1.0, A.mult)
+    ts(cf(4), cf(0), 0.5, A.add, 16384.0, A.mult)
     ts(ci(0), v("KJ", 0, 1), 96, A.bitwise_and)
     cp(cf(3), ci(0))
     ts(v("SEL"), v("SLI"), cf(3), A.is_equal)
-    act(row(0), v("MR", 0, 128, p=(0, 1)), bias=-512.0 * 7.5, scale=-512.0)
-    M2, MS = 1.5 * 2.0 ** 36, 1.5 * 2.0 ** 18
-    for i, c_ in enumerate((M2, -M2, 127.0, 2.0 ** -18, MS, -MS, 10.0 / 32)):
-        act(row(1 + i), one1(128), scale=c_)
-    for i, c_ in enumerate((-15.5, 1.5 * 2.0 ** 28, -1.5 * 2.0 ** 28)):
-        act(row(8 + i), one1(128), scale=c_)
-    act(v("BFN"), BF, scale=-1.0)
-    ts(cf(4), cf(0), 0.5, A.add, 16384.0, A.mult)
-    ms(v("D0"), 1.0 / 32)
-    ms(v("D0", 0, D0W, 8), 512.0)
+    now[0] = "q"
+    b = v(lease(), 0, V)
+    mm(b, [(fl(0, 65), v("FF", 0, V, p=(0, 65)))])
+    lin(v("EC"), b, 1.0, 128.0 - 1.0 / 64)
     cp(v("PU"), v("PI"))
-    cp(v("QU"), v("QI"))
-    cp(LF, v("LI"))
+    for lo, hi in FAVOR_CH:
+        cp(v("LF", lo, hi), v("LI", lo, hi))
     ts(ci(1), v("THI", 0, 1), 4080, A.bitwise_and)
     ts(ci(2), v("THI", 0, 1), 15, A.bitwise_and)
     ts(cf(5), ci(1), -2048.0, A.mult)
     ts(cf(11), ci(2), 0.5, A.add, -2048.0, A.mult)
+    ts(cf(7, p8), v("MGI", 0, 1, p=p8), 0.5, A.add, -512.0, A.mult)
+    cp(v("QU"), v("QI"))
     act(v("DH"), IB, scale=cf(5))
     act(v("DL", 0, 128), IB, scale=cf(11))
-    p8, q8 = (0, 8), (32, 40)
-    ms(v("MH"), 0.0)
-    ts(ci(3, p8), v("MGI", 0, 1, p=p8), 4080, A.bitwise_and)
-    ts(ci(4, q8), v("THI", 2, 3, p=q8), 15, A.bitwise_and)
-    ts(cf(7, p8), ci(3, p8), -512.0, A.mult)
-    ts(cf(8, q8), ci(4, q8), 0.5, A.add, -512.0, A.mult)
-    ts(v("MH", 0, 128, p=p8), v("B8", 0, 128, p=p8), 0.0, A.is_equal, cf(7, p8), A.mult)
-    ts(v("MH", 0, 128, p=q8), v("B8", 0, 128, p=q8), 0.0, A.is_equal, cf(8, q8), A.mult)
+    b = v(lease(), 0, 1)
+    mm(b, [(v("E8", 0, 128, p=p8), cf(7, p8))])
+    act(cf(8), b)
 
-    bank = [0]
+    def window(x, col, w):
+        b = v(lease(), 0, w)
+        o = col % K if w <= K else 0
+        mm(b, [(fl(0, 65), v("FF", o, o + w, p=(0, 65)))], last=False)
+        mm(b, [(IB, x)], first=False, hot=True)
+        lin(v("WW", col, col + w), b, 1.0, 1.0 + (col - o - 2048) * E17)
 
-    def dbank():
-        bank[0] ^= 1
-        return "PD%d" % bank[0]
+    now[0] = "w"
+    for c in range(2):
+        mm(v("PZ%d" % (1 - c), K, V), [(fl(0, 97), v("FF", K * c, K * c + K, p=(0, 97))), (IB, v("XB", K * c, K * c + K))])
+    for j in range(WN // V):
+        window(v("XB", V * j, V * j + V), V * j, V)
 
-    def window(x, col, w, eng="a", where=None):
-        b = v(where or dbank(), 0, w)
-        o = col % 256 if w <= 256 else 0
-        mm(b, [(IB, x), (v("FL", 0, 128, p=(0, 65)), v("FF", o, o + w, p=(0, 65)))])
-        c_ = 1.0 + (col - o - 2048) * E17
-        if eng == "a":
-            act(v("WW", col, col + w), b, bias=c_)
-        else:
-            ts(v("WW", col, col + w), b, c_, A.add)
+    def spread(t):
+        lanes = [x for lo, hi, sub in G1[t] if sub for x in (lo, hi)]
+        a, z = min(lanes), max(lanes)
+        for p_ in range(16):
+            x, y = v("BR", 2048 * (t % 2) + p_, 2048 * (t % 2) + 16 * (z - a), 16), xs_(t - 2, a, z)
+            add({"g": (lambda x=x, y=y: g.affine_select(a_(x), a_(y), [[0, z - a]], A.is_ge, 0.0, 0, 0), 170 + 2 * CYC * (z - a))}, [x], [y])
 
-    tag[0] = "w"
-    for j in range(7):
-        window(v("XB", 512 * j, 512 * j + 512), 512 * j, 512, "av"[j % 2], ("PZ0", "PZ1", "PD0", "PD1")[j % 4])
-    window(v("XB", 3584, 3840), 3584, 256, "v", "PD1")
-    window(v("XB", 3840, 4096), 3840, 256, "a", "PZ0")
-    tag[0] = "i"
-    ts(v("PKB"), v("WW", 0, V), -9.0 / 32, A.add)
-    for lo, hi in ((768, 1280), (1792, 2304), (2560, 4096)):
-        dma("s", T.yx[:, lo:hi], v("XB", lo, hi), 256 * (hi - lo), after=v("WW", WN - 8, WN))
-    tt(v("DB"), v("XB", 0, K), v("XB", K, V), A.subtract)
-
-    if VUPD:
-        iota(v("FI"), [[1, 128]], 0, 0)
-        for t in range(RO - 1):
-            act(v("FR", 128 * t, 128 * t + 128), v("FI"), scale=E17, bias=-127.0 + ((1 + t % (n - 1)) * V + K * (t % 2) + CH[-1][0] - 2048) * E17)
-
-    def prepare(t, keys=False):
+    def lapses(t):
         o = K * (t % 2)
-        old = (lambda a, b: v("XB", o + a, o + b)) if t < 2 else (lambda a, b: v("XS", K * (t - 2) + a, K * (t - 2) + b))
-        if keys:
+        if t < 2:
             cp(v("SU", K * t, K * t + K), v("SI", o, o + K))
-            ts(v("PM3", K, V), v("SI", o, o + K), E17, A.mult, -127.0 - 10.0 / 32 - 1.0 / 64, A.add)
-            tt(v("KO", K * t, K * t + K), v("PM3", K, V), old(0, K), A.add)
-            return
-        b = dbank()
-        for h in range(2):
-            mm(v(b, 128 * h, 128 * h + 128), [(old(128 * h, 128 * h + 128), IB)])
-        act(v("BT", K * t, K * t + K), v(b, 0, K), scale=-1.0)
+            b = v(lease(), 0, K)
+            ts(b, v("SI", o, o + K), E17, A.mult, -127.0 - 10.0 / 32 - 1.0 / 64, A.add)
+            tt(v("KO", K * t, K * t + K), b, v("XB", o, o + K), A.add)
+        win = (v("XB"), v("X1"), WW, WW)[t]
+        own = lambda a, b_: v("XB", o + a, o + b_) if t < 2 else xs_(t - 2, a, b_)
+        at = lambda nm, a, b_: v(nm, WN * t + 16 * a, WN * t + 16 * b_)
+        shift = 127.0 if t > 1 else 0.0
+        halves = sorted(set(lo // 128 for lo, hi, sub in G1[t] if not sub))
+        if t < 2:
+            for h in halves:
+                b = v(lease(), 0, 128)
+                mm(b, [(own(128 * h, 128 * h + 128), IB)])
+                lin(v("BT", K * t + 128 * h, K * t + 128 * h + 128), b, -1.0)
+        else:
+            b = lease()
+            for h in halves:
+                mm(v(b, 128 * h, 128 * h + 128), [(own(128 * h, 128 * h + 128), IB)])
+            lin(v("BT", K * t, K * t + 128 * len(halves)), v(b, 0, 128 * len(halves)), -1.0)
+        a = min([lo for lo, hi, sub in G1[t] if sub] + [K])
+        for lo, hi, sub in G1[t]:
+            src_ = ind(win, v("SU", K * t + lo, K * t + hi))
+            if sub:
+                ae = v("AE", 16 * (lo - a), 16 * (hi - a))
+                tt(ae, src_, v("BR", 2048 * (t % 2) + 16 * (lo - a), 2048 * (t % 2) + 16 * (hi - a)), A.subtract)
+                act(at("AB", lo, hi), ae, FN.Abs, bias=shift)
+                continue
+            lin(at("AA", lo, hi), src_, 1.0, shift)
+            for l0 in range(lo, hi, 32):
+                b, q, h0 = v(lease(), 0, V), (l0 % 128, l0 % 128 + 32), K * t + 128 * (l0 // 128)
+                mm(b, [(v("BT", h0, h0 + 128, p=q), v("SEL", 0, V, p=q))], last=False)
+                mm(b, [(IB, at("AA", l0, l0 + 32))], first=False)
+                act(at("AB", l0, l0 + 32), b, FN.Abs)
+        ec = lambda p_: v("CC", 15 - p_, 143 - p_) if p_ % 2 else v("CC", 160 - p_, 288 - p_)
+        for lo, hi in SUMS[t]:
+            w, u0 = hi - lo, WN * t + 16 * lo
+            terms = ([(ec(p_), v("AB", u0 + p_, u0 + 16 * w, 16)) for p_ in range(16)]
+                     + [(v("DH"), one(w, 128)), (v("DL", 128 * t, 128 * t + 128), one(w, 128))])
+            step = 9 if w <= 64 else STEP
+            for j in range(0, 18, step):
+                mm(v("PZ%d" % (t % 2), lo, hi), terms[j:j + step], j == 0, j + step == 18, t > 1)
+                ops[-1]["wr"].append(("turn%d" % (t % 2), 0, 1, 0, 128))
 
-    prepare(0, True)
-    prepare(0)
-    prepare(1)
+    def settle(t, a, w):
+        z = v("PZ%d" % (t % 2), a, a + w)
+        tt(z, z, v("KO", K * t + a, K * t + a + w), A.max)
+        tt(v("K3", K * t + a, K * t + a + w), z, v("MM", K * t + a, K * t + a + w), A.min)
+
+    def sources(t, a, w):
+        o = K * (t % 2)
+        s = lambda nm, off=K * t: v(nm, off + a, off + a + w)
+        xs, c3 = xs_(t, a, a + w), 127.0 + 10.0 / 32 + 1.0 / 64
+        b = v(lease(), 0, w)
+        mm(b, [(IBN, xs), (fl(1, 33), one(w, 33)), (BN, s("PT"))], last=False)
+        mm(b, [(IF, s("K3"))], first=False)
+        tt(s("HH"), b, s("EC", o), A.max)
+        b = v(lease(), 0, w)
+        mm(b, [(IF, s("HH"))], last=False, hot=t < 2)
+        mm(b, [(fl(0, 1), v("D0", 1, 1 + 4 * w, 4, p=(0, 1))), (row(4), one(w)), (fl(2, 65), one(w, 65))], False, False, t < 2)
+        mm(b, [(IFN, s("HH"))], first=False, hot=t < 2)
+        if t < 2:
+            ts(s("SU", K * (t + 2)), b, c3, A.subtract, -(2.0 ** 17), A.mult)
+            tt(s("KO", K * (t + 2)), xs, b, A.subtract)
+        else:
+            lin(s("SF", o), b, -(2.0 ** 17), c3 * 2.0 ** 17)
+
+    ar, cnt = 0, []
     for t in range(RO):
+        now[0] = str(t)
         c = t % 2
         o, rv, d = K * c, K * (c ^ 1), 1 + t % (n - 1)
         dst, src = T.cores[(rank + d) % n], T.cores[(rank - d) % n]
-        pu = v("PU", 16 * c, 16 * c + 16)
-        tag[0], tag[1] = "r" if t else "q", t
-        act(v("TF"), ind(LF, pu))
+        ts(v("TH"), ind(LF, v("PU", 16 * c, 16 * c + 16)), 2048.0, A.subtract)
+        lin(v("TF"), ind(LF, v("PU", 16 * c, 16 * c + 16)))
+        b = lease()
         for h in range(2):
-            tag[0] = ("r%d" if t or h else "q%d") % h
-            mm(v("PM1", 128 * h, 128 * h + 128), [(v("PM", 256 * h + 128 * u, 256 * h + 128 * u + 128), v("TF", u, K, 2)) for u in range(2)])
-            cp(v("TU", 128 * h, 128 * h + 128), v("PM1", 128 * h, 128 * h + 128))
-        for lo, hi in GA:
-            ts(v("YA", 8 * lo, 8 * hi), ind(WW, v("TU", lo // 2, hi // 2)), -8.0 / 32, A.add)
-        for j, (lo, hi, e) in enumerate(G1):
-            tag[0] = "g%d" % j
-            src_ = ind(WW, v("SU", K * t + lo, K * t + hi))
-            if e == "a":
-                act(v("AA", 16 * lo, 16 * hi), src_, bias=127.0)
-            else:
-                ts(v("AA", 16 * lo, 16 * hi), src_, 127.0, A.add)
-        tag[0] = "h"
-        act(v("Y0"), v("YA", 7, 2048, 8), bias=127.25)
-        hp = v("PM1", K, V)
-        mm(hp, [(BP, v("Y0")), (row(0), one1(K)), (row(1), one1(K)), (row(2), one1(K)), (BN, v("Y0"))])
-        act(v("HM"), hp, FN.Relu, bias=cf(4), scale=32.0)
+            mm(v(b, 128 * h, 128 * h + 128), [(v("PM", 256 * h + 128 * u, 256 * h + 128 * u + 128), v("TH", u, K, 2)) for u in range(2)], hot=True)
+        ts(v("TU"), v(b, 0, K), 2048.0, A.add)
+        for lo, hi in GA[t]:
+            lin(v("YA", 8 * lo, 8 * hi), ind(WW, v("TU", lo // 2, hi // 2)), 1.0, -8.0 / 32)
+        for lo, hi in GB[t]:
+            tt(v("YB", 8 * lo, 8 * hi), ind(WW, v("TU", 128 + lo // 2, 128 + hi // 2)), v("YA", 8 * lo, 8 * hi), A.min)
+        if t > 1:
+            lapses(t)
+        lin(v("Y0"), v("YA", 7, 2048, 8), 1.0, 127.25)
+        hp = v("PS", K, V)
+        mm(hp, [(BP, v("Y0")), (row(0), one(K)), (row(1), one(K)), (row(2), one(K)), (BN, v("Y0"))])
+        act(v("HM"), hp, FN.Relu, cf(4), 32.0)
         tt(v("GG"), ind(LF, v("QU", 16 * c, 16 * c + 16)), v("HM"), A.min)
-        mm(v("PM2", 0, K), [(IFN, v("TF"))], last=False)
-        mm(v("PM2", 0, K), [(BF, v("GG"))], first=False)
-        for ci_, (a, w) in enumerate(CH):
-            zb = "PZ%d" % ((ci_ + t * len(CH)) % 2)
-            end = ci_ == len(CH) - 1
-            for l0 in range(a, a + w, 32):
-                tag[0] = "b%d" % (l0 // 64)
-                b = v(dbank())
-                q = (l0 % 128, l0 % 128 + 32)
-                h0 = K * t + 128 * (l0 // 128)
-                mm(b, [(IB, v("AA", 16 * l0, 16 * l0 + 512)), (v("BT", h0, h0 + 128, p=q), v("SEL", 0, 512, p=q))])
-                act(v("AB", 16 * l0, 16 * l0 + 512), b, FN.Abs)
-                if (l0 + 32 - a) % 64 == 0:
-                    l1 = l0 - 32
-                    ec = lambda p_: v("CC", 15 - p_, 143 - p_) if p_ % 2 else v("CC", 160 - p_, 288 - p_)
-                    mm(v(zb, l1 - a, l1 - a + 64), [(v("DH"), v("ONE", 0, 64)), (v("DL", 128 * t, 128 * t + 128), v("ONE", 0, 64))]
-                       + [(ec(p_), v("AB", 16 * l1 + p_, 16 * l1 + 1024, 16)) for p_ in range(16)])
-            tag[0] = "c%d" % ci_
-            s = lambda nm, off=0: v(nm, off + a, off + a + w)
-            z, zz, kb = v(zb, 0, w), v(zb, K, K + w), s("PKB", o)
-            tt(v("YB", 8 * a, 8 * (a + w)), ind(WW, v("TU", 128 + a // 2, 128 + (a + w) // 2)), v("YA", 8 * a, 8 * (a + w)), A.min)
+        ops[-1]["wr"].append(("turn2", 0, 1, 0, 128))
+        for j, terms in enumerate([[(v("IH"), v("TH")), (row(3), one(K))], [(BF, v("GG"))]]):
+            mm(v("PS", 0, K), terms, j == 0, j == 1)
+            ops[-1]["wr"].append(("turn2", 0, 1, 0, 128))
+        for a, w in CH[t]:
+            s = lambda nm, off=K * t: v(nm, off + a, off + a + w)
             sc, yb, d0 = v("SC", 8 * a, 8 * (a + w)), v("YB", 8 * a, 8 * (a + w)), v("D0", 0, 8 * w)
-            add("v", lambda sc=sc, yb=yb, d0=d0: g.vector.tensor_tensor_scan(sc["ap"], d0["ap"], yb["ap"], 0.0, A.add, A.min), [sc], [yb, d0], 30 + CYC * 8 * w)
-            tt(s("MM"), v("SC", 8 * a + 7, 8 * (a + w), 8), kb, A.min)
-            tt(z, z, s("KO", K * t), A.max)
-            tt(s("K3"), z, s("MM"), A.min)
-            M = 1.5 * 2.0 ** 23
-            ts(s("X2"), s("K3"), M + 127, A.add, M, A.subtract)
-            pre = [(BN if c else BP, s("DB")), (v("MH", 0, 128, p=(0, 40)), v("ONE", 0, w, p=(0, 40))), (BP, s("XS", K * (t - 1)) if t else s("XB", rv))]
-            mm(zz, pre, last=False)
-            mm(zz, [(BN, s("X2"))], first=False)
-            xs = s("XS", K * t)
-            if end and FASTX:
-                tt(s("XT"), zz, s("X2"), A.max)
-                tt(xs, s("XT"), s("XB", o), A.min)
-            tt(s("KT"), zz, s("K3"), A.max)
-            tt(s("K4"), s("KT"), kb, A.min)
-            if not (end and FASTX):
-                ts(xs, s("K4"), M + 127, A.add, M, A.subtract)
-            ar = t * len(CH) + ci_
+            add({"v": (lambda sc=sc, yb=yb, d0=d0: g.vector.tensor_tensor_scan(a_(sc), a_(d0), a_(yb), 0.0, A.add, A.min), vcost(sc, yb))}, [sc], [yb, d0])
+            be = s("XB", o)
+            tt(s("MM"), v("SC", 8 * a + 7, 8 * (a + w), 8), s("PZ%d" % (1 - c), K), A.min)
+            if t > 1:
+                settle(t, a, w)
+            x2 = s("X2", 0)
+            ts(x2, s("K3") if t > 1 else s("MM"), M + 127, A.add, M, A.subtract)
+            zp = v(lease(), 0, w)
+            mm(zp, [(BP, be), (IB, v("ND", t + a, t + a + w))] + ([(BN, s("XB", rv)), (BP, xs_(t - 1, a, a + w))] if t else []), last=False)
+            mm(zp, [(BN, x2)], first=False, hot=True)
+            ts(s("PT"), zp, cf(8), A.add, 0.0, A.is_gt)
+            xs, land = xs_(t, a, a + w), land_(t, a, a + w)
+            b = v(lease(), 0, w)
+            mm(b, [(IB, x2)], last=False, hot=True)
+            mm(b, [(BP, s("PT"))], first=False, hot=True)
+            tt(xs, b, be, A.min)
             rid, pid, _ = topo.addr(dst)
-            land = s("LAND", K * t)
-            add("g", lambda xs=xs, land=land, ar=ar, rid=rid, pid=pid, mk=topo.mask(core, dst):
-                g.remote_dma(land["ap"], xs["ap"], T.sem["ar%d" % ar], T.sem.sent, pid, rid, mk), [], [xs], 300.0, kind="r",
+            add({"g": (lambda xs=xs, land=land, ar=ar, rid=rid, pid=pid, mk=topo.mask(core, dst):
+                       g.remote_dma(a_(land), a_(xs), T.sem["ar%d" % ar], T.sem.sent, pid, rid, mk), 300.0)}, [], [xs], kind="r",
                 extra=len(topo.engines(core, dst)))
-            add(None, None, [land], [], 0.0, lat=REM, kind="arr", extra=(ar, len(topo.engines(src, core)), len(ops) - 1))
+            add({None: (None, 0.0)}, [land], [], lat=REM + 4.0 * w, kind="arr", extra=(ar, len(topo.engines(src, core)), len(ops) - 1))
+            ar += 1
             if t == RO - 1:
-                dma("s", T.yx[:, d * V + o + a:d * V + o + a + w], land, 256 * w)
-                dma("s", T.yx[:, o + a:o + a + w], xs, 256 * w)
-            zp = s("PM3")
-            mm(zp, pre + [(IB, v("ND", t + a, t + a + w))], last=False)
-            mm(zp, [(BN, s("X2"))], first=False)
-            if end and FASTP:
-                ts(s("PT"), zp, 0.0, A.is_gt)
-                if t < RO - 1:
-                    act(s("SG"), s("PT"), acc=v("CNT", ar, ar + 1))
-            else:
-                act(s("SG"), zp, FN.Sign)
-                act(s("PT"), s("SG"), FN.Relu, acc=v("CNT", ar, ar + 1) if t < RO - 1 else None)
-            tt(s("DM"), s("PM2"), s("PT"), A.mult)
-            tt(ind(LF, v("PU", 16 * c + a // 16, 16 * c + (a + w) // 16)), s("TF"), s("DM"), A.add)
-            tag[0] = "s%d" % ci_
-            sp = z
-            c3 = 127.0 + 10.0 / 32 + 1.0 / 64
-            if MAGIC_S:
-                lev = [(IF, s("K4")), (IBN, xs)] + [(row(i), one1(w)) for i in (3, 4, 5, 6, 7)] + [(IFN, s("K4"))]
-                if t < 2 and KOACT:
-                    ko = s("KO", K * (t + 2))
-                    mm(sp, lev)
-                    act(ko, sp, scale=-1.0)
-                    mm(sp, [(IFN, ko), (IB, xs)])
-                    ts(s("SU", K * (t + 2)), sp, c3, A.subtract, -(2.0 ** 17), A.mult)
-                elif t < 2:
-                    mm(sp, lev + [(IB, xs)])
-                    ts(s("SU", K * (t + 2)), sp, c3, A.subtract, -(2.0 ** 17), A.mult)
-                    tt(s("KO", K * (t + 2)), xs, sp, A.subtract)
-                else:
-                    mm(sp, lev + [(IB, xs)])
-                    act(s("SF", o), sp, bias=c3 * 2.0 ** 17, scale=-(2.0 ** 17))
-            else:
-                ts(s("I1"), s("K4"), 2.0 ** 17, A.mult, 2048.0, A.add)
-                ts(s("I2"), s("I1"), 4095, A.bitwise_and)
-                if t < 2:
-                    cp(s("SU", K * (t + 2)), s("I2"))
-                    ts(sp, s("I2"), E17, A.mult, -c3, A.add)
-                    tt(s("KO", K * (t + 2)), sp, xs, A.add)
-                else:
-                    cp(s("SF", o), s("I2"))
-            if t == RO - 1:
-                dma("a", T.ys[:, o + a:o + a + w], s("SF", o), 512 * w)
+                sources(t, a, w)
+        if t == RO - 1:
+            dma(T.yx[:, d * V + o:d * V + o + K], land_(t, 0, K), 65536)
+            dma(T.yx[:, K:V], xs_(t, 0, K), 65536)
+            dma(T.ys[:, K:V], v("SF", K, V), 131072)
+        if t < 2:
+            spread(t + 2)
+        for a, w in CH[t]:
+            tt(v("DM", a, a + w), v("PS", a, a + w), v("PT", K * t + a, K * t + a + w), A.mult)
+            tt(ind(LF, v("PU", 16 * c + a // 16, 16 * c + (a + w) // 16)), v("TF", a, a + w), v("DM", a, a + w), A.add)
         if t < RO - 1:
-            a, w = CH[-1]
-            tag[0] = "u0"
-            window(v("LAND", K * t, K * t + a), d * V + o, a)
-            window(v("XS", K * t, K * t + K), o, K)
-            if t < 2:
-                prepare(t + 2)
-            tag[0] = "k"
-            if t == 0:
-                prepare(1, True)
-            tag[0] = "u1"
-            if VUPD:
-                tt(v("WW", d * V + o + a, d * V + o + K), v("LAND", K * t + a, K * t + K), v("FR", 128 * t, 128 * t + w), A.add)
-            else:
-                window(v("LAND", K * t + a, K * t + K), d * V + o + a, w)
-            tag[0] = "e"
-            dma("s", T.yx[:, d * V + o:d * V + o + K], v("LAND", K * t, K * t + K), 65536)
-            nc = (t + 1) * len(CH)
-            act(v("CJ", 0, nc), v("CNT", 0, nc), acc=cf(10))
-            mm(v("PM3", K, K + 1), [(BF, cf(10)), (row(8), one1(1)), (row(9), one1(1)), (row(10), one1(1)), (v("BFN"), cf(10))])
-            act(cf(9), v("PM3", K, K + 1), bias=cf(11), scale=2048.0)
-            act(v("DL", 128 * (t + 1), 128 * (t + 2)), IB, scale=cf(9))
+            window(xs_(t, 0, K), o, K)
+            for a, w in CH[t]:
+                window(land_(t, a, a + w), d * V + o + a, w)
+            dma(T.yx[:, d * V + o:d * V + o + K], land_(t, 0, K), 65536)
+        if t < 2:
+            lapses(t)
+            for a, w in LATE[t]:
+                settle(t, a, w)
+                sources(t, a, w)
         if t == 2:
-            dma("s", T.yx[:, 0:K], v("XS", K * t, K * t + K), 65536)
-            dma("s", T.ys[:, 0:K], v("SF", 0, K), 131072)
-    dma("s", T.yl[:, 0:V], v("LF", 0, V), 262144)
-    dma("a", T.yl[:, V:NS], v("LF", V, NS), 262144)
+            sources(t, 0, K)
+        if t < RO - 1:
+            cnt.append(v("CNT", t, t + 1))
+            act(v("CJ"), v("PT", K * t, K * t + K), acc=cnt[-1])
+            b = v(lease(), 0, 1)
+            for j, x in enumerate(cnt):
+                mm(b, [(BF, x)], j == 0, False)
+            mm(b, [(row(5), one(1)), (row(6), one(1)), (row(7), one(1))], False, False)
+            for j, x in enumerate(cnt):
+                mm(b, [(v("BFN"), x)], False, j == len(cnt) - 1)
+            lin(cf(9), b, 2048.0, cf(11))
+            lin(v("DL", 128 * (t + 1), 128 * (t + 2)), IB, cf(9))
+        if t == 0:
+            for lo, hi in ((768, 1280), (1792, 2304), (2560, 4096)):
+                dma(T.yx[:, lo:hi], v("XB", lo, hi), 256 * (hi - lo), after=land_(0, 0, K))
+        if t == 2:
+            dma(T.yx[:, 0:K], xs_(t, 0, K), 65536)
+            dma(T.ys[:, 0:K], v("SF", 0, K), 131072)
+    dma(T.yl[:], LF, 524288)
     return ops
 
 
@@ -416,175 +452,157 @@ def depend(ops):
     for i, op in enumerate(ops):
         dp = set()
         for wr, regs in ((False, op["rd"]), (True, op["wr"])):
-            for nm, lo, hi in regs:
-                ps = SCRATCH[nm][0] == "psum"
-                for j, w2, l2, h2 in hist.get(nm, []):
-                    if j != i and (((wr or w2) and lo < h2 and l2 < hi) or (ps and ops[j]["eng"] != op["eng"])):
-                        dp.add(j)
+            for nm, lo, hi, p, q in regs:
+                dp.update(j for j, w2, l2, h2, p2, q2 in hist.get(nm, []) if j != i and (wr or w2) and lo < h2 and l2 < hi and p < q2 and p2 < q)
         if op["kind"] == "arr":
             dp.add(op["x"][2])
         for wr, regs in ((False, op["rd"]), (True, op["wr"])):
-            for nm, lo, hi in regs:
+            for nm, lo, hi, p, q in regs:
                 h = hist.setdefault(nm, [])
-                if wr and SCRATCH[nm][0] != "psum":
-                    h[:] = [e for e in h if not (lo <= e[2] and e[3] <= hi)]
-                if SCRATCH[nm][0] == "psum" and h and ops[h[-1][0]]["eng"] != op["eng"]:
-                    k = len(h)
-                    while k and ops[h[k - 1][0]]["eng"] == ops[h[-1][0]]["eng"]:
-                        k -= 1
-                    del h[:k]
-                h.append((i, wr, lo, hi))
+                if wr:
+                    h[:] = [e for e in h if not (lo <= e[2] and e[3] <= hi and p <= e[4] and e[5] <= q)]
+                h.append((i, wr, lo, hi, p, q))
         deps.append(dp)
     return deps
 
 
-def schedule(ops, deps, cost=COST, fixed=None):
-    n, LAT, BW = len(ops), cost[4], cost[6]
+def lines(ops):
+    where = {op["tag"]: i for i, op in enumerate(ops) if op["tag"]}
+    named, out = set(), {}
+    for e, text in ORDER.items():
+        t, out[e] = "p", []
+        for w in text.split():
+            if w[0] == "@":
+                t = w[1:]
+            else:
+                out[e].append(w if w[0] == "*" or ":" in w else w + ":" + t)
+        named.update(out[e])
+    for e in ORDER:
+        q = []
+        for w in out[e]:
+            q += [i for tag, i in where.items() if tag.endswith(":" + w[1:]) and tag not in named and e in ops[i]["ways"]] if w[0] == "*" else [where[w]]
+        out[e] = q
+    assert sorted(out["v"] + out["a"]) == sorted(where.values()), sorted(set(where) - set(ops[i]["tag"] for i in out["v"] + out["a"]))
+    out["g"] = [i for i, op in enumerate(ops) if "g" in op["ways"]]
+    return out
+
+
+def schedule(ops, deps0):
+    n, fixed = len(ops), lines(ops)
+    eng = [next(iter(op["ways"])) for op in ops]
+    place = {}
+    for e, q in fixed.items():
+        for k, i in enumerate(q):
+            eng[i], place[i] = e, k
+    psum = [next((r[0] for r in op["rd"] + op["wr"] if r[0][:5] == "lease" or SCRATCH.get(r[0], "s")[0] == "psum"), None) for op in ops]
+    member = {}
+    for i in range(n):
+        if psum[i] and psum[i] not in SCRATCH:
+            member.setdefault(psum[i], []).append(i)
     succ = [[] for _ in ops]
-    for i, dp in enumerate(deps):
+    for i, dp in enumerate(deps0):
         for j in dp:
             succ[j].append(i)
-    prio = [0.0] * n
-    for i in range(n - 1, -1, -1):
-        op = ops[i]
-        prio[i] = op["dur"] + op["lat"] + (op["x"] / BW if op["kind"] == "d" else 0) + max([prio[j] + LAT for j in succ[i]] + [0.0])
-    prio = [p + URGENT.get(op["tag"], 0.0) for p, op in zip(prio, ops)]
-    left = [len(dp) for dp in deps]
-    ready = [i for i in range(n) if not left[i]]
-    free, done, start, order, fed = {e: 0.0 for e in ("dma", "v", "a", "p", "g", "s", None)}, [0.0] * n, [0.0] * n, [], [0.0] * n
-    while ready:
-        if fixed:
-            i = fixed[len(order)]
-            s0 = max(free[ops[i]["eng"]], fed[i])
-        else:
-            st = {i: max(free[ops[i]["eng"]], fed[i]) for i in ready}
-            m = min(ready, key=lambda i: st[i] + ops[i]["dur"])
-            cand = [i for i in ready if ops[i]["eng"] == ops[m]["eng"] and st[i] <= st[m] + LOOK * ops[m]["dur"]]
-            loads = [i for i in cand if ops[i]["kind"] == "d" and not deps[i]]
-            i = min(loads) if loads else max(cand, key=lambda i: (prio[i], -i))
-            s0 = st[i]
-        op = ops[i]
-        start[i] = s0
-        if op["eng"]:
-            free[op["eng"]] = s0 + op["dur"]
-        done[i] = s0 + op["dur"] + op["lat"]
-        if op["kind"] == "d":
-            free["dma"] = done[i] = max(done[i], free["dma"]) + op["x"] / BW
-        order.append(i)
-        ready.remove(i)
-        for j in succ[i]:
-            left[j] -= 1
-            fed[j] = max(fed[j], done[i] + (0.0 if op["eng"] == "p" == ops[j]["eng"] else LAT))
-            if not left[j]:
-                ready.append(j)
-    return order, start, done
+    dur = [ops[i]["ways"][eng[i]][1] for i in range(n)]
+    due, best = [float(i) for i in range(n)], None
+    for turn in range(PASSES):
+        deps, left = [set(d) for d in deps0], [len(d) for d in deps0]
+        head, free = {e: 0 for e in fixed}, {e: 0.0 for e in ("dma", "v", "a", "p", "g", "s", None)}
+        ready = set(i for i in range(n) if not left[i])
+        bank, holder, last, togo = {}, {b: None for b in POOL}, {}, {u: len(m) for u, m in member.items()}
+        begin, done, order = [0.0] * n, [0.0] * n, []
 
+        def start(i):
+            e, nm, take = eng[i], psum[i], None
+            after = []
+            if nm in SCRATCH or nm in bank:
+                after = [j for e2, j in last.get(bank.get(nm, nm), {}).items() if e2 != e]
+            elif nm:
+                user = next(j for j in member[nm] if eng[j] != "p")
+                idle = [b for b in POOL if holder[b] is None]
+                near = place[user] - head[eng[user]]
+                if not turn:
+                    return max([free[e]] + [done[j] + WAKE for j in deps[i]]), None, []
+                if (near > AHEAD and ops[user]["tag"][-1] != "w") or len(idle) <= (0 if near == 0 else 1):
+                    return None
+                take = min(idle, key=lambda b: max([done[j] for j in last.get(b, {}).values()] + [0.0]))
+                after = list(last.get(take, {}).values())
+            return max([free[e]] + [done[j] + (-60.0 if eng[j] == e == "p" else 0.0 if e is None else WAKE) for j in list(deps[i]) + after]), take, after
 
-def place(ops, deps, cost=COST, passes=6):
-    n, LAT, BW = len(ops), cost[4], cost[6]
-    succ = [[] for _ in ops]
-    for i, dp in enumerate(deps):
-        for j in dp:
-            succ[j].append(i)
-    isd = [op["kind"] == "d" for op in ops]
-    res = ["dma" if isd[i] else ops[i]["eng"] for i in range(n)]
-    dur = [ops[i]["x"] / BW if isd[i] else ops[i]["dur"] for i in range(n)]
-    pre = [ops[i]["lat"] if isd[i] else 0.0 for i in range(n)]
-    post = [0.0 if isd[i] else ops[i]["lat"] for i in range(n)]
-
-    def sweep(prio, before, after, pre, post):
-        left = [len(x) for x in before]
-        ready, fed, st, busy = [i for i in range(n) if not left[i]], [0.0] * n, [0.0] * n, {}
         while ready:
-            i = max(ready, key=lambda i: prio[i])
+            st = {i: start(i) for i in ready if eng[i] not in fixed or place[i] == head[eng[i]]}
+            st = {i: x for i, x in st.items() if x}
+            m = min(st, key=lambda i: (st[i][0], due[i]))
+            i = min((j for j in st if eng[j] == eng[m] and st[j][0] <= st[m][0] + min(LOOK, dur[m])), key=lambda j: (due[j], j))
+            i = min([j for j in st if eng[j] == eng[m] and ops[j].get("hot") and st[j][0] < st[i][0] + dur[i]] or [i], key=lambda j: (st[j][0], due[j]))
+            s0, take, after = st[i]
+            e, op = eng[i], ops[i]
+            deps[i].update(after)
+            begin[i], done[i] = s0, s0 + dur[i] + op["lat"]
+            if e and (turn or e != "p"):
+                free[e] = s0 + dur[i]
+            if e in fixed:
+                head[e] += 1
+            if op["kind"] == "d":
+                free["dma"] = done[i] = max(s0 + DLAT, free["dma"]) + op["x"] / BW
+            if take:
+                bank[psum[i]], holder[take], last[take] = take, psum[i], {}
+            if psum[i] and turn:
+                last.setdefault(bank.get(psum[i], psum[i]), {})[e] = i
+                if psum[i] in togo:
+                    togo[psum[i]] -= 1
+                    if not togo[psum[i]]:
+                        holder[bank[psum[i]]] = None
+            order.append(i)
             ready.remove(i)
-            t = fed[i] + pre[i]
-            if res[i]:
-                b = busy.setdefault(res[i], [])
-                k = 0
-                while k < len(b) and b[k][0] < t + dur[i]:
-                    t = max(t, b[k][1])
-                    k += 1
-                b.insert(k, (t, t + dur[i]))
-            st[i] = t
-            for j in after[i]:
+            for j in succ[i]:
                 left[j] -= 1
-                fed[j] = max(fed[j], t + dur[i] + (0.0 if res[i] == "p" == res[j] else post[i] + LAT))
                 if not left[j]:
-                    ready.append(j)
-        return st
-
-    prio = [0.0] * n
-    for i in range(n - 1, -1, -1):
-        prio[i] = pre[i] + dur[i] + post[i] + max([prio[j] + LAT for j in succ[i]] + [0.0])
-    first = [i for i in range(n) if isd[i] and not deps[i]]
-    best = None
-    for _ in range(passes):
-        prio = [p + URGENT.get(op["tag"], 0.0) for p, op in zip(prio, ops)]
-        for i in first:
-            prio[i] = 1e9 - i
-        st = sweep(prio, deps, succ, pre, post)
-        order = sorted(range(n), key=lambda i: (-1.0, i) if i in first else (st[i] - pre[i], i))
-        span = max(schedule(ops, deps, cost, order)[2])
-        if best is None or span < best[0]:
-            best = (span, order)
-        back = sweep([st[i] + dur[i] for i in range(n)], succ, deps, post, pre)
-        prio = [back[i] + dur[i] for i in range(n)]
-    return best[1]
-
-
-def arrange(ops, deps):
-    pos = [(op["t"] * PERIOD + SLOT.get(op["tag"], 0), i) for i, op in enumerate(ops)]
-    succ = [[] for _ in ops]
-    left = [len(dp) for dp in deps]
-    for i, dp in enumerate(deps):
-        for j in dp:
-            succ[j].append(i)
-    for e in "vapgs":
-        q = sorted(p for p in pos if ops[p[1]]["eng"] == e)
-        for (_, i), (_, j) in zip(q, q[1:]):
-            succ[i].append(j)
-            left[j] += 1
-    order = [i for i in range(len(ops)) if not left[i]]
-    for i in order:
-        for j in succ[i]:
-            left[j] -= 1
-            if not left[j]:
-                order.append(j)
-    assert len(order) == len(ops)
-    return order
+                    ready.add(j)
+        assert len(order) == n
+        if turn and (best is None or max(done) < best[-1]):
+            best = (order, eng, deps, bank, max(done))
+        for i in range(n - 1, -1, -1):
+            if ops[i]["kind"] == "d" and not deps0[i]:
+                continue
+            tail = dur[i] + ops[i]["lat"] + (DLAT + ops[i]["x"] / BW if ops[i]["kind"] == "d" else 0.0)
+            due[i] = min([begin[i] if eng[i] in fixed else 1e9] + [(begin[j] if eng[j] in fixed else due[j]) - tail - WAKE for j in succ[i]] + [max(done) - tail])
+    return best
 
 
 def rank_program(g, core, T, topo):
     if T.rank_of(core) is None:
         return
-    ops = plan(g, core, T, topo)
-    deps = depend(ops)
-    order = arrange(ops, deps)
+    bank = {}
+    ops = plan(g, core, T, topo, bank)
+    if not KEPT:
+        KEPT["order"] = schedule(ops, depend(ops))
+    order, eng, deps, banks, _ = KEPT["order"]
+    bank.update(banks)
     queue = {"v": g.vector, "a": g.scalar, "p": g.tensor, "g": g, "s": g.sync}
-    skip = lambda i, j: ops[i]["kind"] == "arr" or (ops[i]["eng"] == "p" and ops[j]["eng"] == "p")
+    skip = lambda i, j: ops[i]["kind"] == "arr" or eng[i] == eng[j] == "p"
     needed = set(j for i, dp in enumerate(deps) for j in dp if not skip(i, j))
     count, mark, know, seen, nd = {}, {}, {}, {e: {} for e in queue}, 0
     for i in order:
-        op = ops[i]
+        op, e = ops[i], eng[i]
         if op["kind"] == "arr":
             mark[i], know[i] = ("ar%d" % op["x"][0], op["x"][1]), {}
             count[mark[i][0]] = mark[i][1]
             continue
-        k = seen[op["eng"]]
+        k = seen[e]
         for j in sorted((j for j in deps[i] if not skip(i, j)), key=lambda j: -mark[j][1]):
             s, c = mark[j]
             if k.get(s, 0) < c:
-                queue[op["eng"]].wait_ge(T.sem[s], c)
+                queue[e].wait_ge(T.sem[s], c)
                 k[s] = c
                 for s2, c2 in know[j].items():
                     k[s2] = max(k.get(s2, 0), c2)
-        if op["eng"] == "g" and op["kind"] == "c":
+        if e == "g" and op["kind"] == "c":
             needed.add(i)
             if k.get("sg", 0) < count.get("sg", 0):
                 g.wait_ge(T.sem.sg, count["sg"])
                 k["sg"] = count["sg"]
-        ins = op["fn"]()
+        ins = op["ways"][e][0]()
         know[i] = dict(k)
         if op["kind"] == "r":
             count["sent"] = count.get("sent", 0) + op["x"]
@@ -594,7 +612,7 @@ def rank_program(g, core, T, topo):
             ins.then_inc(T.sem[s], 16)
             mark[i], count[s] = (s, 16), 16
         elif i in needed:
-            s = "s" + op["eng"]
+            s = "s" + e
             ins.then_inc(T.sem[s], 1)
             count[s] = count.get(s, 0) + 1
             mark[i] = (s, count[s])

from concourse.mybir import AluOpType, ActivationFunctionType

K, V, WN, NS, RO = 256, 512, 4096, 1024, 4
CH = [[(0, 192), (192, 64)]] * 4
GA = [[(0, 64), (64, 128), (128, 256)]] * 4
GB = [[(0, 128), (128, 256)]] * 4
G1 = [[(32 * j, 32 * j + 32, False) for j in range(8)]] * 2 + [[(0, 64, False), (64, 128, False), (128, 160, False), (160, 192, True), (192, 256, True)]] * 2
SUMS = [[(0, 128), (128, 256)]] * 2 + [[(0, 64), (64, 128), (128, 192), (192, 256)]] * 2
LATE = [[(0, 256)], [(0, 128), (128, 128)]]
BASE_CH = [(0, 1536), (1536, 1536), (3072, 1024)]
FAVOR_CH = [(0, 768), (768, 1024)]
LOADS = ["src0", "base", "grant", "favor", "th", "mg", "part", "src1", "second"]
POOL = ["P0", "P1", "P2", "P3", "P4"]
ORDER = {
    "v": "*p @w WW1 BT0:0 SU0:0 WW0 PU0:q L0:0 KO0:0 AA0:0 LF0:q LF1:q CI0:q TH0:0 CF2:q TF0:0 CI1:q TU0:0 QU0:q CF0:q "
         "@0 YA0 CF1:q YB0 YB1 SC0 GG0 MM0 X20 SC1 PT0 MM1 X21 XS0 DM0 PT1 L0:1 XS1 DM1 LF0 LF1 BT0:1 WW0 TH0:1 SU0:1 KO0:1 TU0:1 "
         "@1 YA0 CF0:0 YB0 YB1 SC0 GG0 MM0 X20 SC1 PT0 MM1 X21 XS0 PT1 DM0 XS1 DM1 LF0 LF1 TH0:2 ZM0:0 DL0:0 K30:0 TU0:2 WW2 WW1 "
         "@2 YA0 HH0:0 YB0 SU1:0 YB1 AA5:1 Y00 KO1:0 CF0:1 AE1 GG0 SC1 DL0:1 AE0 SC0 MM0 ZM0 K30 MM1 X20 TF0 ZM1 PT0 K31 X21 XS0 PT1 DM0 XS1 "
         "ZM0:1 LF0 K30:1 DM1 LF1 DL0 TH0:3 HH0:1 BT0:3 TU0:3 WW1 SU1:1 "
         "@3 YA0 ZM1:1 K31:1 HH0:2 KO1:1 HH1:1 YB0 SU2:1 Y00 YB1 AE0 SC0 KO2:1 MM0 AE1 GG0 ZM0 K30 X20 SC1 ZM1 PT0 MM1 K31 X21 DM0 XS0 PT1 LF0 XS1 "
         "DM1 LF1 HH0 HH1 SF0 SF1",
    "a": "*p @q EC0 WW2:w BT1:0 WW5:w WW3:w AA1:0 WW6:w WW4:w AB1:0 AB0:0 WW7:w AA2:0 "
         "@0 YA1 YA2 Y00 CF3:q AA4 DL0:q AA3 HM0 AA5 AA6 AB5 AA7 AB2 AB4 AB3 DH0:q AB7 CJ0 AB6 WW1 WW2 "
         "@1 YA1 YA2 Y00 AA0 BT1 AA3 AB0 HM0 AA1 BT0:2 TF0 AA2 AA4 CJ0 WW0 AB4 AB2 AB1 "
         "@2 YA1 AB3:1 YA2 AA0 AA1 AA2 HM0 AB1 AB0 AB3 AB2 AB4 AB5 AB6 AA6:1 AB5:1 AA7:1 AB6:1 CJ0 AB7:1 CF0 WW0 WW2 "
         "@3 YA1 YA2 AA0 AA1 AB0 AB1 AA2 AB5 AB2 AB3 AB4 HM0 AB6 TF0 SF0:2",
}
E17 = 2.0 ** -17
NCH = sum(len(c) for c in CH)

SCRATCH = {
    "XB": ("sbuf", [128, WN], "bfloat16"), "X1": ("sbuf", [128, WN], "bfloat16"),
    "XS": ("sbuf", [128, RO * K], "bfloat16"), "LAND": ("sbuf", [128, RO * K], "bfloat16"),
    "WW": ("sbuf", [128, WN], "float32"), "LI": ("sbuf", [128, NS], "int32"), "LF": ("sbuf", [128, NS], "float32"),
    "SI": ("sbuf", [128, V], "int32"), "SU": ("sbuf", [128, RO * K], "uint16"), "SF": ("sbuf", [128, V], "float32"),
    "PI": ("sbuf", [128, 32], "int32"), "QI": ("sbuf", [128, 32], "int32"), "PU": ("sbuf", [128, 32], "uint16"), "QU": ("sbuf", [128, 32], "uint16"),
    "AA": ("sbuf", [128, RO * WN], "bfloat16"), "AB": ("sbuf", [128, RO * WN], "bfloat16"),
    "YA": ("sbuf", [128, 2048], "float32"), "YB": ("sbuf", [128, 2048], "float32"), "SC": ("sbuf", [128, 2048], "float32"),
    "D0": ("sbuf", [128, 8 * max(w for c in CH for _, w in c)], "bfloat16"), "TF": ("sbuf", [128, K], "float32"), "TU": ("sbuf", [128, K], "uint16"),
    "KO": ("sbuf", [128, RO * K], "float32"), "MM": ("sbuf", [128, RO * K], "float32"), "K3": ("sbuf", [128, RO * K], "float32"),
    "HH": ("sbuf", [128, RO * K], "float32"), "PT": ("sbuf", [128, RO * K], "bfloat16"), "X2": ("sbuf", [128, K], "bfloat16"),
    "Y0": ("sbuf", [128, K], "bfloat16"), "HM": ("sbuf", [128, K], "float32"), "GG": ("sbuf", [128, K], "float32"), "DM": ("sbuf", [128, K], "float32"),
    "EC": ("sbuf", [128, V], "float32"), "CNT": ("sbuf", [128, 16], "float32"), "CJ": ("sbuf", [128, K], "bfloat16"),
    "KJ": ("sbuf", [128, 260], "int32"), "KA": ("sbuf", [128, 260], "int32"), "ND": ("sbuf", [128, 260], "bfloat16"),
    "MR": ("sbuf", [128, 128], "float32"), "SB": ("sbuf", [128, 128], "float32"), "SB2": ("sbuf", [128, 128], "float32"),
    "ZF": ("sbuf", [128, 128], "float32"), "E8": ("sbuf", [128, 128], "float32"),
    "IB": ("sbuf", [128, 128], "bfloat16"), "IBN": ("sbuf", [128, 128], "bfloat16"), "IF": ("sbuf", [128, 128], "float32"), "IFN": ("sbuf", [128, 128], "float32"),
    "BP": ("sbuf", [128, 128], "bfloat16"), "BN": ("sbuf", [128, 128], "bfloat16"), "BF": ("sbuf", [128, 128], "float32"), "BFN": ("sbuf", [128, 128], "float32"),
    "CC": ("sbuf", [128, 288], "bfloat16"), "PM": ("sbuf", [128, 512], "float16"), "FF": ("sbuf", [128, 512], "bfloat16"), "FL": ("sbuf", [128, 384], "bfloat16"),
    "ONE": ("sbuf", [128, K], "bfloat16"), "RW": ("sbuf", [128, 9 * 128], "bfloat16"),
    "TH": ("sbuf", [128, K], "float16"), "IH": ("sbuf", [128, 128], "float16"), "LV": ("sbuf", [128, K], "bfloat16"),
    "THI": ("sbuf", [128, 4], "int32"), "MGI": ("sbuf", [128, 4], "int32"), "CI": ("sbuf", [128, 16], "int32"), "CF": ("sbuf", [128, 16], "float32"),
    "BT": ("sbuf", [128, RO * K], "bfloat16"), "SLI": ("sbuf", [128, V], "int32"), "SEL": ("sbuf", [128, V], "bfloat16"),
    "BR": ("sbuf", [128, WN], "bfloat16"), "AE": ("sbuf", [128, 2048], "float32"),
    "DH": ("sbuf", [128, 128], "bfloat16"), "DL": ("sbuf", [128, RO * 128], "bfloat16"),
}
for _b in POOL + ["PZ0", "PZ1", "PS"]:
    SCRATCH[_b] = ("psum", [128, 512], "float32")
NDMA = 40
SEMAPHORES = ["sv", "sa", "sp", "sg", "sent"] + ["dm%d" % i for i in range(NDMA)] + ["ar%d" % i for i in range(NCH)]
ESZ = {"bfloat16": 2, "float16": 2, "uint16": 2, "float32": 4, "int32": 4}
A = AluOpType
FN = ActivationFunctionType
CYC, PEC, GAT, SCA, WAKE, REM, DLAT, BW = 1.0, 0.5, 1.56, 3.8, 100.0, 2200.0, 1400.0, 220.0
ROWS = 50000
LOOK, AHEAD, STEP, PASSES = 400.0, 3, 3, 2
KEPT = {}


def plan(g, core, T, topo, bank):
    rank, n = T.rank_of(core), len(T.cores)
    ops, leases, now, seen = [], [0], ["p"], {}

    def v(name, lo=None, hi=None, step=1, p=(0, 128)):
        where, shape, kind = SCRATCH.get(name, SCRATCH["P0"])
        if lo is None:
            lo, hi = 0, shape[1]
        return {"at": (name, p, lo, hi, step), "reg": [(name, lo, hi) + p], "n": len(range(lo, hi, step)), "sz": ESZ[kind], "ps": where == "psum"}

    def lease():
        leases[0] += 1
        return "lease%d" % leases[0]

    def ind(win, off):
        return {"win": win, "idx": off, "reg": win["reg"], "off": off["reg"], "n": 16 * off["n"], "sz": 4, "ps": False}

    def a_(x):
        if not isinstance(x, dict):
            return x
        if "win" in x:
            return a_(x["win"]).indirect(a_(x["idx"]))
        name, p, lo, hi, step = x["at"]
        t_ = T[bank.get(name, name)]
        return t_[p[0]:p[1], lo:hi:step] if step != 1 else t_[p[0]:p[1], lo:hi]

    def add(ways, outs, ins, lat=0.0, kind="c", extra=None):
        rd, wr = [], []
        for x in ins:
            if isinstance(x, dict):
                rd += x["reg"] + x.get("off", [])
        for x in outs:
            wr += x["reg"]
            rd += x.get("off", [])
        ops.append({"ways": ways, "rd": rd, "wr": wr, "lat": lat, "kind": kind, "x": extra, "tag": None})
        if "v" in ways or "a" in ways:
            nm = wr[0][0]
            nm = "L" if nm[:5] == "lease" else "ZM" if nm[:2] == "PZ" else "XS" if nm == "X1" else nm
            seen[nm, now[0]] = seen.get((nm, now[0]), -1) + 1
            ops[-1]["tag"] = "%s%d:%s" % (nm, seen[nm, now[0]], now[0])

    def vcost(out, x, two=1.0):
        if "win" in out:
            return 50 + SCA * CYC * out["n"]
        if "win" in x:
            return 50 + GAT * CYC * x["n"]
        return 30 + CYC * max(64, x["n"] * two * (0.5 if out["sz"] == 2 and x["sz"] == 2 and two == 1.0 else 1))

    def ts_(out, x, s1, op0, s2=None, op1=None):
        if op1 is None:
            return lambda: g.vector.tensor_scalar(a_(out), a_(x), a_(s1), None, op0), vcost(out, x)
        return lambda: g.vector.tensor_scalar(a_(out), a_(x), a_(s1), a_(s2), op0, op1), vcost(out, x)

    def act_(out, x, func=FN.Identity, bias=0.0, scale=1.0, acc=None):
        cost = 60 + CYC * max(64, x["n"] * (GAT if "win" in x else 1))
        if acc is None:
            return lambda: g.scalar.activation(a_(out), a_(x), func, bias=a_(bias), scale=a_(scale)), cost
        return lambda: g.scalar.activation(a_(out), a_(x), func, bias=a_(bias), scale=a_(scale), accum_out=a_(acc)), cost + 20

    def ts(out, x, s1, op0, s2=None, op1=None):
        add({"v": ts_(out, x, s1, op0, s2, op1)}, [out], [x, s1, s2])

    def act(out, x, func=FN.Identity, bias=0.0, scale=1.0, acc=None):
        add({"a": act_(out, x, func, bias, scale, acc)}, [out] + ([acc] if acc else []), [x, bias, scale])

    def lin(out, x, scale=1.0, bias=0.0):
        add({"a": act_(out, x, bias=bias, scale=scale), "v": ts_(out, x, scale, A.mult, bias, A.add)}, [out], [x, scale, bias])

    def tt(out, x, y, op):
        add({"v": (lambda: g.vector.tensor_tensor(a_(out), a_(x), a_(y), op), vcost(out, x, 1.0001 if x["ps"] or y["ps"] else 2.0))}, [out], [x, y])

    def cp(out, x):
        add({"v": (lambda: g.vector.tensor_copy(a_(out), a_(x)), vcost(out, x))}, [out], [x])

    def ms(out, c):
        add({"v": (lambda: g.vector.memset(a_(out), c), vcost(out, out))}, [out], [])

    def mm(out, terms, first=True, last=True, hot=False):
        def fn():
            r = None
            for i, (l, x) in enumerate(terms):
                r = g.tensor.matmul(a_(out), a_(l), a_(x), first and i == 0, last and i == len(terms) - 1)
            return r
        add({"p": (fn, sum(PEC * max(64, x["n"]) * (4 if x["sz"] == 4 else 1) for _, x in terms))}, [out], [y for t_ in terms for y in t_], lat=60.0)
        ops[-1]["hot"] = hot

    def iota(out, pat, base, cm):
        if SCRATCH[out["reg"][0][0]][2] == "int32":
            fn = lambda: g.iota(a_(out), pat, base, cm)
        else:
            fn = lambda: g.iota(a_(out), pat, base, cm, allow_small_or_imprecise_dtypes=True)
        add({"g": (fn, 130 + 2 * CYC * out["n"])}, [out], [])

    def dma(out, x, nbytes, after=None):
        add({"s": (lambda: g.sync.dma_start(a_(out), a_(x)), 60.0)}, [out] if isinstance(out, dict) else [], [x, after], kind="d", extra=nbytes + ROWS)

    row = lambda i: v("RW", 128 * i, 128 * i + 128, p=(0, 1))
    one = lambda w, k=1: v("ONE", 0, w, p=(0, k))
    fl = lambda j, k: v("FL", 128 * j, 128 * j + 128, p=(0, k))
    cf = lambda i, p=(0, 128): v("CF", i, i + 1, p=p)
    ci = lambda i, p=(0, 128): v("CI", i, i + 1, p=p)
    IB, IBN, IF, IFN, BP, BN, BF = (v(x) for x in ("IB", "IBN", "IF", "IFN", "BP", "BN", "BF"))
    WW, LF = v("WW"), v("LF")
    p8 = (0, 8)
    xs_ = lambda t, a, b: v("X1", a, b) if t == 0 else v("XS", K * t + a, K * t + b)
    land_ = lambda t, a, b: v("X1", V + a, V + b) if t == 0 else v("LAND", K * t + a, K * t + b)

    loads = {
        "src0": [(v("SI", 0, K), T.src[:, 0:K], 131072)], "src1": [(v("SI", K, V), T.src[:, K:V], 131072)],
        "base": [(v("XB", lo, lo + w), T.base[:, lo:lo + w], 256 * w) for lo, w in BASE_CH],
        "grant": [(v("PI"), T.grant[:], 16384)], "part": [(v("QI"), T.part[:], 16384)], "favor": [(v("LI", lo, hi), T.favor[:, lo:hi], 512 * (hi - lo)) for lo, hi in FAVOR_CH],
        "th": [(v("THI", 0, 1), T.th[:], 8192)], "mg": [(v("MGI", 0, 1, p=p8), T.mg[:], 512)],
        "second": [(v("X1", lo, hi), T.base[:, lo:hi], 256 * (hi - lo)) for lo, hi in ((K, V), (V + K, WN))],
    }
    for name in LOADS:
        for out, x, nb in loads[name]:
            dma(out, x, nb)

    M2, MS, MA, M = 1.5 * 2.0 ** 36, 1.5 * 2.0 ** 18, 1.5 * 2.0 ** 28, 1.5 * 2.0 ** 23
    ms(v("FF"), 1.0)
    ms(v("FL"), 0.0)
    ms(v("ONE"), 1.0)
    ms(v("ZF"), 0.0)
    ms(v("FF", 0, 256, p=(64, 65)), 0.0)
    ms(v("CC"), 0.0)
    zb, zf, blocks = v("FL", 256, 384), v("ZF"), [[-16, 8], [0, 16]]

    def pick(out, x, pat, op, c_, base=0, cm=1):
        add({"g": (lambda: g.affine_select(a_(out), a_(x), pat, op, c_, base, cm), 170 + 2 * CYC * out["n"])}, [out], [x])

    def band(out, x, c_):
        pick(out, x, blocks, A.is_ge, c_, -16)
        pick(out, out, blocks, A.is_ge, 0.0)

    iota(v("KJ"), [[-1, 260]], 1024, 1)
    iota(v("FF", 0, 512, p=(0, 1)), [[0, 2], [1, 256]], 0, 0)
    band(BF, zf, 1.0)
    iota(v("MR"), [[0, 8], [1, 16]], 0, 0)
    iota(v("SLI"), [[-1, 32], [0, 16]], 0, 1)
    pick(v("E8", 0, 128, p=p8), v("ZF", 0, 128, p=p8), [[-1, 8], [0, 16]], A.not_equal, 1.0)
    band(BP, zb, 512.0)
    band(BN, zb, -512.0)
    for i, c_ in enumerate((M2, -M2, -2048.0, MS, -15.5, MA, -MA)):
        pick(row(1 + i), one(128), [[0, 128]], A.is_gt, c_, 0, 0)
    band(v("BFN"), zf, -1.0)
    for out, x, c_ in ((IBN, zb, -1.0), (IF, zf, 1.0), (IFN, zf, -1.0)):
        pick(out, x, [[-1, 128]], A.not_equal, c_)
    for j, rows in enumerate(((E17, -128.0, 2.0 ** -9, 45.0 / 64), (127.0, 11.0 / 32), (-MS, 127.0, 10.0 / 32))):
        for i, c_ in enumerate(rows):
            out, x = v("FL", 128 * j, 128 * j + 128, p=(32 * i, 32 * i + 1)), v("ONE", 0, 128, p=(32 * i, 32 * i + 1))
            if j:
                pick(out, x, [[0, 128]], A.is_gt, c_, 0, 0)
            else:
                act(out, x, scale=c_)
    ts(IB, v("KJ", 0, 128), 1024.0, A.is_equal)
    ts(v("KA"), v("KJ"), 15, A.bitwise_and)
    cp(cf(0), v("KA", 0, 1))
    ms(v("D0"), 1.0 / 32)
    ms(v("D0", 0, SCRATCH["D0"][1][1], 8), 512.0)
    ts(v("ND"), v("KA"), 0.0, A.not_equal, -(2.0 ** 23), A.mult)
    act(v("CC", 15, 143, 16), v("BF", 0, 128, 16), scale=2048.0)
    act(v("CC", 160, 288, 16), v("BF", 0, 128, 16), scale=2048.0)
    act(row(0), v("MR", 0, 128, p=(0, 1)), bias=-512.0 * 7.5, scale=-512.0)
    ts(v("SB2"), v("MR"), cf(0), A.add, 1.0, A.add)
    tt(v("SB"), v("SB2"), BF, A.mult)
    ts(cf(1), cf(0), 8.0, A.is_lt)
    ts(cf(2), cf(0), 8.0, A.is_ge)
    ts(v("PM", 0, 128), v("SB"), 8.0, A.is_equal)
    ts(v("PM", 128, 256), v("SB"), 16.0, A.is_equal, cf(1), A.mult)
    ts(v("PM", 256, 384), v("SB"), 16.0, A.is_equal, cf(2), A.mult)
    ts(v("PM", 384, 512), v("SB"), 24.0, A.is_equal)
    ts(v("IH"), v("KJ", 0, 128), 1024.0, A.is_equal, -1.0, A.mult)
    ts(cf(4), cf(0), 0.5, A.add, 16384.0, A.mult)
    ts(ci(0), v("KJ", 0, 1), 96, A.bitwise_and)
    cp(cf(3), ci(0))
    ts(v("SEL"), v("SLI"), cf(3), A.is_equal)
    now[0] = "q"
    b = v(lease(), 0, V)
    mm(b, [(fl(0, 65), v("FF", 0, V, p=(0, 65)))])
    lin(v("EC"), b, 1.0, 128.0 - 1.0 / 64)
    cp(v("PU"), v("PI"))
    for lo, hi in FAVOR_CH:
        cp(v("LF", lo, hi), v("LI", lo, hi))
    ts(ci(1), v("THI", 0, 1), 4080, A.bitwise_and)
    ts(ci(2), v("THI", 0, 1), 15, A.bitwise_and)
    ts(cf(5), ci(1), -2048.0, A.mult)
    ts(cf(11), ci(2), 0.5, A.add, -2048.0, A.mult)
    ts(cf(7, p8), v("MGI", 0, 1, p=p8), 0.5, A.add, -512.0, A.mult)
    cp(v("QU"), v("QI"))
    act(v("DH"), IB, scale=cf(5))
    act(v("DL", 0, 128), IB, scale=cf(11))
    b = v(lease(), 0, 1)
    mm(b, [(v("E8", 0, 128, p=p8), cf(7, p8))])
    act(cf(8), b)

    def window(x, col, w):
        b = v(lease(), 0, w)
        o = col % K if w <= K else 0
        mm(b, [(fl(0, 65), v("FF", o, o + w, p=(0, 65)))], last=False)
        mm(b, [(IB, x)], first=False, hot=True)
        lin(v("WW", col, col + w), b, 1.0, 1.0 + (col - o - 2048) * E17)

    now[0] = "w"
    for c in range(2):
        mm(v("PZ%d" % (1 - c), K, V), [(fl(0, 97), v("FF", K * c, K * c + K, p=(0, 97))), (IB, v("XB", K * c, K * c + K))])
    for j in range(WN // V):
        window(v("XB", V * j, V * j + V), V * j, V)

    def spread(t):
        lanes = [x for lo, hi, sub in G1[t] if sub for x in (lo, hi)]
        a, z = min(lanes), max(lanes)
        for p_ in range(16):
            x, y = v("BR", 2048 * (t % 2) + p_, 2048 * (t % 2) + 16 * (z - a), 16), xs_(t - 2, a, z)
            add({"g": (lambda x=x, y=y: g.affine_select(a_(x), a_(y), [[0, z - a]], A.is_ge, 0.0, 0, 0), 170 + 2 * CYC * (z - a))}, [x], [y])

    def lapses(t):
        o = K * (t % 2)
        if t < 2:
            cp(v("SU", K * t, K * t + K), v("SI", o, o + K))
            b = v(lease(), 0, K)
            ts(b, v("SI", o, o + K), E17, A.mult, -127.0 - 10.0 / 32 - 1.0 / 64, A.add)
            tt(v("KO", K * t, K * t + K), b, v("XB", o, o + K), A.add)
        win = (v("XB"), v("X1"), WW, WW)[t]
        own = lambda a, b_: v("XB", o + a, o + b_) if t < 2 else xs_(t - 2, a, b_)
        at = lambda nm, a, b_: v(nm, WN * t + 16 * a, WN * t + 16 * b_)
        shift = 127.0 if t > 1 else 0.0
        halves = sorted(set(lo // 128 for lo, hi, sub in G1[t] if not sub))
        if t < 2:
            for h in halves:
                b = v(lease(), 0, 128)
                mm(b, [(own(128 * h, 128 * h + 128), IB)])
                lin(v("BT", K * t + 128 * h, K * t + 128 * h + 128), b, -1.0)
        else:
            b = lease()
            for h in halves:
                mm(v(b, 128 * h, 128 * h + 128), [(own(128 * h, 128 * h + 128), IB)])
            lin(v("BT", K * t, K * t + 128 * len(halves)), v(b, 0, 128 * len(halves)), -1.0)
        a = min([lo for lo, hi, sub in G1[t] if sub] + [K])
        for lo, hi, sub in G1[t]:
            src_ = ind(win, v("SU", K * t + lo, K * t + hi))
            if sub:
                ae = v("AE", 16 * (lo - a), 16 * (hi - a))
                tt(ae, src_, v("BR", 2048 * (t % 2) + 16 * (lo - a), 2048 * (t % 2) + 16 * (hi - a)), A.subtract)
                act(at("AB", lo, hi), ae, FN.Abs, bias=shift)
                continue
            lin(at("AA", lo, hi), src_, 1.0, shift)
            for l0 in range(lo, hi, 32):
                b, q, h0 = v(lease(), 0, V), (l0 % 128, l0 % 128 + 32), K * t + 128 * (l0 // 128)
                mm(b, [(v("BT", h0, h0 + 128, p=q), v("SEL", 0, V, p=q))], last=False)
                mm(b, [(IB, at("AA", l0, l0 + 32))], first=False)
                act(at("AB", l0, l0 + 32), b, FN.Abs)
        ec = lambda p_: v("CC", 15 - p_, 143 - p_) if p_ % 2 else v("CC", 160 - p_, 288 - p_)
        for lo, hi in SUMS[t]:
            w, u0 = hi - lo, WN * t + 16 * lo
            terms = ([(ec(p_), v("AB", u0 + p_, u0 + 16 * w, 16)) for p_ in range(16)]
                     + [(v("DH"), one(w, 128)), (v("DL", 128 * t, 128 * t + 128), one(w, 128))])
            step = 9 if w <= 64 else STEP
            for j in range(0, 18, step):
                mm(v("PZ%d" % (t % 2), lo, hi), terms[j:j + step], j == 0, j + step == 18, t > 1)
                ops[-1]["wr"].append(("turn%d" % (t % 2), 0, 1, 0, 128))

    def settle(t, a, w):
        z = v("PZ%d" % (t % 2), a, a + w)
        tt(z, z, v("KO", K * t + a, K * t + a + w), A.max)
        tt(v("K3", K * t + a, K * t + a + w), z, v("MM", K * t + a, K * t + a + w), A.min)

    def sources(t, a, w):
        o = K * (t % 2)
        s = lambda nm, off=K * t: v(nm, off + a, off + a + w)
        xs, c3 = xs_(t, a, a + w), 127.0 + 10.0 / 32 + 1.0 / 64
        b = v(lease(), 0, w)
        mm(b, [(IBN, xs), (fl(1, 33), one(w, 33)), (BN, s("PT"))], last=False)
        mm(b, [(IF, s("K3"))], first=False)
        tt(s("HH"), b, s("EC", o), A.max)
        b = v(lease(), 0, w)
        mm(b, [(IF, s("HH"))], last=False, hot=t < 2)
        mm(b, [(fl(0, 1), v("D0", 1, 1 + 4 * w, 4, p=(0, 1))), (row(4), one(w)), (fl(2, 65), one(w, 65))], False, False, t < 2)
        mm(b, [(IFN, s("HH"))], first=False, hot=t < 2)
        if t < 2:
            ts(s("SU", K * (t + 2)), b, c3, A.subtract, -(2.0 ** 17), A.mult)
            tt(s("KO", K * (t + 2)), xs, b, A.subtract)
        else:
            lin(s("SF", o), b, -(2.0 ** 17), c3 * 2.0 ** 17)

    ar, cnt = 0, []
    for t in range(RO):
        now[0] = str(t)
        c = t % 2
        o, rv, d = K * c, K * (c ^ 1), 1 + t % (n - 1)
        dst, src = T.cores[(rank + d) % n], T.cores[(rank - d) % n]
        ts(v("TH"), ind(LF, v("PU", 16 * c, 16 * c + 16)), 2048.0, A.subtract)
        lin(v("TF"), ind(LF, v("PU", 16 * c, 16 * c + 16)))
        b = lease()
        for h in range(2):
            mm(v(b, 128 * h, 128 * h + 128), [(v("PM", 256 * h + 128 * u, 256 * h + 128 * u + 128), v("TH", u, K, 2)) for u in range(2)], hot=True)
        ts(v("TU"), v(b, 0, K), 2048.0, A.add)
        for lo, hi in GA[t]:
            lin(v("YA", 8 * lo, 8 * hi), ind(WW, v("TU", lo // 2, hi // 2)), 1.0, -8.0 / 32)
        for lo, hi in GB[t]:
            tt(v("YB", 8 * lo, 8 * hi), ind(WW, v("TU", 128 + lo // 2, 128 + hi // 2)), v("YA", 8 * lo, 8 * hi), A.min)
        if t > 1:
            lapses(t)
        lin(v("Y0"), v("YA", 7, 2048, 8), 1.0, 127.25)
        hp = v("PS", K, V)
        mm(hp, [(BP, v("Y0")), (row(0), one(K)), (row(1), one(K)), (row(2), one(K)), (BN, v("Y0"))])
        act(v("HM"), hp, FN.Relu, cf(4), 32.0)
        tt(v("GG"), ind(LF, v("QU", 16 * c, 16 * c + 16)), v("HM"), A.min)
        ops[-1]["wr"].append(("turn2", 0, 1, 0, 128))
        for j, terms in enumerate([[(v("IH"), v("TH")), (row(3), one(K))], [(BF, v("GG"))]]):
            mm(v("PS", 0, K), terms, j == 0, j == 1)
            ops[-1]["wr"].append(("turn2", 0, 1, 0, 128))
        for a, w in CH[t]:
            s = lambda nm, off=K * t: v(nm, off + a, off + a + w)
            sc, yb, d0 = v("SC", 8 * a, 8 * (a + w)), v("YB", 8 * a, 8 * (a + w)), v("D0", 0, 8 * w)
            add({"v": (lambda sc=sc, yb=yb, d0=d0: g.vector.tensor_tensor_scan(a_(sc), a_(d0), a_(yb), 0.0, A.add, A.min), vcost(sc, yb))}, [sc], [yb, d0])
            be = s("XB", o)
            tt(s("MM"), v("SC", 8 * a + 7, 8 * (a + w), 8), s("PZ%d" % (1 - c), K), A.min)
            if t > 1:
                settle(t, a, w)
            x2 = s("X2", 0)
            ts(x2, s("K3") if t > 1 else s("MM"), M + 127, A.add, M, A.subtract)
            zp = v(lease(), 0, w)
            mm(zp, [(BP, be), (IB, v("ND", t + a, t + a + w))] + ([(BN, s("XB", rv)), (BP, xs_(t - 1, a, a + w))] if t else []), last=False)
            mm(zp, [(BN, x2)], first=False, hot=True)
            ts(s("PT"), zp, cf(8), A.add, 0.0, A.is_gt)
            xs, land = xs_(t, a, a + w), land_(t, a, a + w)
            b = v(lease(), 0, w)
            mm(b, [(IB, x2)], last=False, hot=True)
            mm(b, [(BP, s("PT"))], first=False, hot=True)
            tt(xs, b, be, A.min)
            rid, pid, _ = topo.addr(dst)
            add({"g": (lambda xs=xs, land=land, ar=ar, rid=rid, pid=pid, mk=topo.mask(core, dst):
                       g.remote_dma(a_(land), a_(xs), T.sem["ar%d" % ar], T.sem.sent, pid, rid, mk), 300.0)}, [], [xs], kind="r",
                extra=len(topo.engines(core, dst)))
            add({None: (None, 0.0)}, [land], [], lat=REM + 4.0 * w, kind="arr", extra=(ar, len(topo.engines(src, core)), len(ops) - 1))
            ar += 1
            if t == RO - 1:
                sources(t, a, w)
        if t == RO - 1:
            dma(T.yx[:, d * V + o:d * V + o + K], land_(t, 0, K), 65536)
            dma(T.yx[:, K:V], xs_(t, 0, K), 65536)
            dma(T.ys[:, K:V], v("SF", K, V), 131072)
        if t < 2:
            spread(t + 2)
        for a, w in CH[t]:
            tt(v("DM", a, a + w), v("PS", a, a + w), v("PT", K * t + a, K * t + a + w), A.mult)
            tt(ind(LF, v("PU", 16 * c + a // 16, 16 * c + (a + w) // 16)), v("TF", a, a + w), v("DM", a, a + w), A.add)
        if t < RO - 1:
            window(xs_(t, 0, K), o, K)
            for a, w in CH[t]:
                window(land_(t, a, a + w), d * V + o + a, w)
            dma(T.yx[:, d * V + o:d * V + o + K], land_(t, 0, K), 65536)
        if t < 2:
            lapses(t)
            for a, w in LATE[t]:
                settle(t, a, w)
                sources(t, a, w)
        if t == 2:
            sources(t, 0, K)
        if t < RO - 1:
            cnt.append(v("CNT", t, t + 1))
            act(v("CJ"), v("PT", K * t, K * t + K), acc=cnt[-1])
            b = v(lease(), 0, 1)
            for j, x in enumerate(cnt):
                mm(b, [(BF, x)], j == 0, False)
            mm(b, [(row(5), one(1)), (row(6), one(1)), (row(7), one(1))], False, False)
            for j, x in enumerate(cnt):
                mm(b, [(v("BFN"), x)], False, j == len(cnt) - 1)
            lin(cf(9), b, 2048.0, cf(11))
            lin(v("DL", 128 * (t + 1), 128 * (t + 2)), IB, cf(9))
        if t == 0:
            for lo, hi in ((768, 1280), (1792, 2304), (2560, 4096)):
                dma(T.yx[:, lo:hi], v("XB", lo, hi), 256 * (hi - lo), after=land_(0, 0, K))
        if t == 2:
            dma(T.yx[:, 0:K], xs_(t, 0, K), 65536)
            dma(T.ys[:, 0:K], v("SF", 0, K), 131072)
    dma(T.yl[:], LF, 524288)
    return ops


def depend(ops):
    hist, deps = {}, []
    for i, op in enumerate(ops):
        dp = set()
        for wr, regs in ((False, op["rd"]), (True, op["wr"])):
            for nm, lo, hi, p, q in regs:
                dp.update(j for j, w2, l2, h2, p2, q2 in hist.get(nm, []) if j != i and (wr or w2) and lo < h2 and l2 < hi and p < q2 and p2 < q)
        if op["kind"] == "arr":
            dp.add(op["x"][2])
        for wr, regs in ((False, op["rd"]), (True, op["wr"])):
            for nm, lo, hi, p, q in regs:
                h = hist.setdefault(nm, [])
                if wr:
                    h[:] = [e for e in h if not (lo <= e[2] and e[3] <= hi and p <= e[4] and e[5] <= q)]
                h.append((i, wr, lo, hi, p, q))
        deps.append(dp)
    return deps


def lines(ops):
    where = {op["tag"]: i for i, op in enumerate(ops) if op["tag"]}
    named, out = set(), {}
    for e, text in ORDER.items():
        t, out[e] = "p", []
        for w in text.split():
            if w[0] == "@":
                t = w[1:]
            else:
                out[e].append(w if w[0] == "*" or ":" in w else w + ":" + t)
        named.update(out[e])
    for e in ORDER:
        q = []
        for w in out[e]:
            q += [i for tag, i in where.items() if tag.endswith(":" + w[1:]) and tag not in named and e in ops[i]["ways"]] if w[0] == "*" else [where[w]]
        out[e] = q
    assert sorted(out["v"] + out["a"]) == sorted(where.values()), sorted(set(where) - set(ops[i]["tag"] for i in out["v"] + out["a"]))
    out["g"] = [i for i, op in enumerate(ops) if "g" in op["ways"]]
    return out


def schedule(ops, deps0):
    n, fixed = len(ops), lines(ops)
    eng = [next(iter(op["ways"])) for op in ops]
    place = {}
    for e, q in fixed.items():
        for k, i in enumerate(q):
            eng[i], place[i] = e, k
    psum = [next((r[0] for r in op["rd"] + op["wr"] if r[0][:5] == "lease" or SCRATCH.get(r[0], "s")[0] == "psum"), None) for op in ops]
    member = {}
    for i in range(n):
        if psum[i] and psum[i] not in SCRATCH:
            member.setdefault(psum[i], []).append(i)
    succ = [[] for _ in ops]
    for i, dp in enumerate(deps0):
        for j in dp:
            succ[j].append(i)
    dur = [ops[i]["ways"][eng[i]][1] for i in range(n)]
    due, best = [float(i) for i in range(n)], None
    for turn in range(PASSES):
        deps, left = [set(d) for d in deps0], [len(d) for d in deps0]
        head, free = {e: 0 for e in fixed}, {e: 0.0 for e in ("dma", "v", "a", "p", "g", "s", None)}
        ready = set(i for i in range(n) if not left[i])
        bank, holder, last, togo = {}, {b: None for b in POOL}, {}, {u: len(m) for u, m in member.items()}
        begin, done, order = [0.0] * n, [0.0] * n, []

        def start(i):
            e, nm, take = eng[i], psum[i], None
            after = []
            if nm in SCRATCH or nm in bank:
                after = [j for e2, j in last.get(bank.get(nm, nm), {}).items() if e2 != e]
            elif nm:
                user = next(j for j in member[nm] if eng[j] != "p")
                idle = [b for b in POOL if holder[b] is None]
                near = place[user] - head[eng[user]]
                if not turn:
                    return max([free[e]] + [done[j] + WAKE for j in deps[i]]), None, []
                if (near > AHEAD and ops[user]["tag"][-1] != "w") or len(idle) <= (0 if near == 0 else 1):
                    return None
                take = min(idle, key=lambda b: max([done[j] for j in last.get(b, {}).values()] + [0.0]))
                after = list(last.get(take, {}).values())
            return max([free[e]] + [done[j] + (-60.0 if eng[j] == e == "p" else 0.0 if e is None else WAKE) for j in list(deps[i]) + after]), take, after

        while ready:
            st = {i: start(i) for i in ready if eng[i] not in fixed or place[i] == head[eng[i]]}
            st = {i: x for i, x in st.items() if x}
            m = min(st, key=lambda i: (st[i][0], due[i]))
            i = min((j for j in st if eng[j] == eng[m] and st[j][0] <= st[m][0] + min(LOOK, dur[m])), key=lambda j: (due[j], j))
            i = min([j for j in st if eng[j] == eng[m] and ops[j].get("hot") and st[j][0] < st[i][0] + dur[i]] or [i], key=lambda j: (st[j][0], due[j]))
            s0, take, after = st[i]
            e, op = eng[i], ops[i]
            deps[i].update(after)
            begin[i], done[i] = s0, s0 + dur[i] + op["lat"]
            if e and (turn or e != "p"):
                free[e] = s0 + dur[i]
            if e in fixed:
                head[e] += 1
            if op["kind"] == "d":
                free["dma"] = done[i] = max(s0 + DLAT, free["dma"]) + op["x"] / BW
            if take:
                bank[psum[i]], holder[take], last[take] = take, psum[i], {}
            if psum[i] and turn:
                last.setdefault(bank.get(psum[i], psum[i]), {})[e] = i
                if psum[i] in togo:
                    togo[psum[i]] -= 1
                    if not togo[psum[i]]:
                        holder[bank[psum[i]]] = None
            order.append(i)
            ready.remove(i)
            for j in succ[i]:
                left[j] -= 1
                if not left[j]:
                    ready.add(j)
        assert len(order) == n
        if turn and (best is None or max(done) < best[-1]):
            best = (order, eng, deps, bank, max(done))
        for i in range(n - 1, -1, -1):
            if ops[i]["kind"] == "d" and not deps0[i]:
                continue
            tail = dur[i] + ops[i]["lat"] + (DLAT + ops[i]["x"] / BW if ops[i]["kind"] == "d" else 0.0)
            due[i] = min([begin[i] if eng[i] in fixed else 1e9] + [(begin[j] if eng[j] in fixed else due[j]) - tail - WAKE for j in succ[i]] + [max(done) - tail])
    return best


def rank_program(g, core, T, topo):
    if T.rank_of(core) is None:
        return
    bank = {}
    ops = plan(g, core, T, topo, bank)
    if not KEPT:
        KEPT["order"] = schedule(ops, depend(ops))
    order, eng, deps, banks, _ = KEPT["order"]
    bank.update(banks)
    queue = {"v": g.vector, "a": g.scalar, "p": g.tensor, "g": g, "s": g.sync}
    skip = lambda i, j: ops[i]["kind"] == "arr" or eng[i] == eng[j] == "p"
    needed = set(j for i, dp in enumerate(deps) for j in dp if not skip(i, j))
    count, mark, know, seen, nd = {}, {}, {}, {e: {} for e in queue}, 0
    for i in order:
        op, e = ops[i], eng[i]
        if op["kind"] == "arr":
            mark[i], know[i] = ("ar%d" % op["x"][0], op["x"][1]), {}
            count[mark[i][0]] = mark[i][1]
            continue
        k = seen[e]
        for j in sorted((j for j in deps[i] if not skip(i, j)), key=lambda j: -mark[j][1]):
            s, c = mark[j]
            if k.get(s, 0) < c:
                queue[e].wait_ge(T.sem[s], c)
                k[s] = c
                for s2, c2 in know[j].items():
                    k[s2] = max(k.get(s2, 0), c2)
        if e == "g" and op["kind"] == "c":
            needed.add(i)
            if k.get("sg", 0) < count.get("sg", 0):
                g.wait_ge(T.sem.sg, count["sg"])
                k["sg"] = count["sg"]
        ins = op["ways"][e][0]()
        know[i] = dict(k)
        if op["kind"] == "r":
            count["sent"] = count.get("sent", 0) + op["x"]
        elif op["kind"] == "d":
            s = "dm%d" % nd
            nd += 1
            ins.then_inc(T.sem[s], 16)
            mark[i], count[s] = (s, 16), 16
        elif i in needed:
            s = "s" + e
            ins.then_inc(T.sem[s], 1)
            count[s] = count.get(s, 0) + 1
            mark[i] = (s, count[s])
    for s, c in count.items():
        g.wait_ge(T.sem[s], c)
